import numpy as np
import ml_dtypes


def mxq(x, axis, fmt="e4m3"):
    dtype, down = {"e4m3": (ml_dtypes.float8_e4m3fn, 7), "e5m2": (ml_dtypes.float8_e5m2, 14)}[fmt]
    v = np.moveaxis(np.asarray(x, np.float32).astype(ml_dtypes.bfloat16).astype(np.float64), axis, -1)
    blocks = v.reshape(v.shape[:-1] + (-1, 32))
    amax = np.abs(blocks).max(-1, keepdims=True)
    byte = np.maximum(np.where(amax > 0, np.frexp(amax)[1] - 1 + 127, 0) - down, 1)
    scale = np.exp2(byte - 127.0)
    codes = (blocks / scale).astype(np.float32).astype(dtype).astype(np.float64)
    return np.moveaxis((codes * scale).reshape(v.shape), -1, axis)


WIDE = False


def mx_kscale(k):
    if not WIDE:
        return np.ones(k)
    levels = np.array([10, -10, 5, -5, 0])
    if k % 512:
        return np.exp2(np.random.permutation(np.resize(levels, k // 32))).repeat(32)
    a = np.empty((k // 512, 16))
    for p in range(k // 512):
        a[p, :8] = np.random.permutation(np.resize(levels, 8))
        for g in range(8):
            far = levels[np.abs(levels - a[p, g]) >= 10]
            a[p, g + 8] = far[np.random.randint(len(far))]
    return np.exp2(a.ravel()).repeat(32)


def f64(x):
    return np.asarray(x).astype(np.float64)


def striped(idx):
    return np.tile(idx.reshape(-1, 16).T, (8, 1)).astype(np.uint16)


def unstriped(offs):
    return offs[:16].T.reshape(-1).astype(np.int64)


E2M1 = np.array([0.0, 0.5, 1.0, 1.5, 2.0, 3.0, 4.0, 6.0, -0.0, -0.5, -1.0, -1.5, -2.0, -3.0, -4.0, -6.0])


def pack_weight(w, fmt):
    k, n = w.shape
    w = f64(np.asarray(w, np.float32).astype(ml_dtypes.bfloat16)).reshape(k // 32, 32, n)
    amax = np.abs(w).max(1)
    if fmt == "e4m3":
        byte = np.frexp(amax)[1] - 1 + 127 - 7
    else:
        mant, ex = np.frexp(amax / 6.0)
        byte = np.where(mant > 0.5, ex, ex - 1) + 127
    byte = np.clip(np.where(amax > 0, byte, 1), 1, 254)
    scaled = (w * np.exp2(127.0 - byte)[:, None, :]).reshape(k, n).astype(np.float32)
    by_word = np.ascontiguousarray(scaled.reshape(k // 512, 128, 4, n).transpose(0, 1, 3, 2))
    if fmt == "e4m3":
        words = by_word.astype(ml_dtypes.float8_e4m3fn).view(np.uint8)
    else:
        c = by_word.astype(ml_dtypes.float4_e2m1fn).view(np.uint8) & 0xF
        words = (c[..., 0::2] | (c[..., 1::2] << 4)).reshape(k // 512, 128, 2 * n)
    return np.ascontiguousarray(words), np.ascontiguousarray(byte.astype(np.uint8).reshape(k // 512, 16, n))


def unpack_weight(words, scales, fmt):
    g, _, n = scales.shape
    words = np.ascontiguousarray(words).reshape(g, 128, n, -1)
    if fmt == "e4m3":
        vals = words.view(ml_dtypes.float8_e4m3fn).astype(np.float64)
    else:
        nib = np.empty((g, 128, n, 4), np.uint8)
        nib[..., 0::2] = words & 0xF
        nib[..., 1::2] = words >> 4
        vals = E2M1[nib]
    vals = vals * np.repeat(np.exp2(scales.astype(np.float64) - 127.0), 8, axis=1)[..., None]
    return vals.transpose(0, 1, 3, 2).reshape(g * 512, n)


def sigmoid(v):
    return 1.0 / (1.0 + np.exp(-np.maximum(v, -700.0)))


K, T, E, C, H, N = 512, 512, 8, 128, 512, 384
R = 2


def by_expert(wq, xq):
    return np.concatenate([wq[e].T @ xq[:, e * C:(e + 1) * C] for e in range(E)], axis=1)


def setup_inputs():
    n = np.random.standard_normal
    s = mx_kscale(K)[:, None]
    u = mx_kscale(H)
    slot_token = np.concatenate([r * (T // R) + np.random.permutation(T // R)[:C // R] for e in range(E) for r in range(R)])
    w1 = [pack_weight(m, "e2m1") for m in n((E, K, H)) / np.sqrt(K) / s[None]]
    w3 = [pack_weight(m, "e2m1") for m in n((E, K, H)) / np.sqrt(K) / s[None] * u[None, None, :]]
    w2 = [pack_weight(m, "e2m1") for m in n((E, H, N)) / np.sqrt(H) / u[None, :, None]]
    return {
        "xT": (n((K, T)) * s).astype(np.float32),
        "w1_words": np.stack([m[0] for m in w1]),
        "w1_scales": np.stack([m[1] for m in w1]),
        "w3_words": np.stack([m[0] for m in w3]),
        "w3_scales": np.stack([m[1] for m in w3]),
        "w2_words": np.stack([m[0] for m in w2]),
        "w2_scales": np.stack([m[1] for m in w2]),
        "offs": striped(slot_token),
    }


def reference(xT, w1_words, w1_scales, w3_words, w3_scales, w2_words, w2_scales, offs):
    idx = unstriped(offs)
    w1 = np.stack([unpack_weight(w1_words[e], w1_scales[e], "e2m1") for e in range(E)])
    w3 = np.stack([unpack_weight(w3_words[e], w3_scales[e], "e2m1") for e in range(E)])
    w2 = np.stack([unpack_weight(w2_words[e], w2_scales[e], "e2m1") for e in range(E)])
    xq = mxq(f64(xT)[:, idx], 0, "e4m3")
    h = sigmoid(by_expert(w1, xq))
    h = h * by_expert(w3, xq)
    y = by_expert(w2, mxq(h, 0, "e4m3"))
    return y.reshape(N, E, R, C // R).transpose(0, 2, 1, 3).reshape(N, E * C)

@@ -1,0 +1,236 @@
+from contextlib import ExitStack
+
+import concourse.mybir as mybir
+from concourse.masks import make_identity
+
+P = 128
+PACK = 4
+K, T, E, C, H, N = 512, 512, 8, 128, 512, 384
+R = 2
+SLOTS = E * C
+N_TILES = N // P
+FLOPS = 2 * SLOTS * (2 * K * H + H * N)
+
+F32 = mybir.dt.float32
+BF16 = mybir.dt.bfloat16
+I32 = mybir.dt.int32
+U32 = mybir.dt.uint32
+U16 = mybir.dt.uint16
+U8 = mybir.dt.uint8
+FP8X4 = mybir.dt.float8_e4m3fn_x4
+FP4X4 = mybir.dt.float4_e2m1fn_x4
+MULT = mybir.AluOpType.mult
+SIGMOID = mybir.ActivationFunctionType.Sigmoid
+
+X_CHUNK = 256
+VECTOR_TOKENS = 176
+
+
+def tile_moe_eps_glu_sigmoid_kernel(
+    tc, xT, w1_words, w1_scales, w3_words, w3_scales, w2_words, w2_scales, offs, out
+):
+    nc = tc.nc
+    with ExitStack() as ctx:
+        keep = ctx.enter_context(tc.tile_pool(name="keep", bufs=1))
+        work = ctx.enter_context(tc.tile_pool(name="work", bufs=3))
+        sigs = ctx.enter_context(tc.tile_pool(name="sigs", bufs=8))
+        psum = ctx.enter_context(tc.psum_pool(name="psum", bufs=2))
+
+        offsets = keep.tile([P, SLOTS // 16], U16, name="offsets")
+        x_raw = [keep.tile([P, PACK, X_CHUNK], F32, name=f"x_raw{c}") for c in range(T // X_CHUNK)]
+        x_grouped = keep.tile([P, T, PACK], BF16, name="x_grouped", align_bytes=64)
+        x_codes = keep.tile([P, T], U32, name="x_codes", align_bytes=64)
+        x_scales = keep.tile([P, T], U8, name="x_scales", align_bytes=64)
+        s_codes = keep.tile([P, SLOTS], U32, name="s_codes", align_bytes=64)
+        s_scales = keep.tile([P, SLOTS], U8, name="s_scales", align_bytes=64)
+        w1_sc = keep.tile([P, E, H], U8, name="w1_sc", align_bytes=64)
+        w3_sc = keep.tile([P, E, H], U8, name="w3_sc", align_bytes=64)
+        w2_sc = keep.tile([P, E, N], U8, name="w2_sc", align_bytes=64)
+        ident = keep.tile([P, P], F32, name="ident")
+        warm = keep.tile([P, 8], F32, name="warm")
+        warm_out = keep.tile([P, 8], F32, name="warm_out")
+
+        nc.sync.dma_start(offsets[:], offs)
+        for c in range(T // X_CHUNK):
+            nc.sync.dma_start(
+                out=x_raw[c][:],
+                in_=xT[:, c * X_CHUNK : (c + 1) * X_CHUNK].rearrange("(p j) w -> p j w", j=PACK),
+            )
+
+        nc.vector.memset(warm[:], 0.0)
+        nc.scalar.activation(warm_out[:], warm[:], SIGMOID)
+        nc.vector.memset(w1_sc[:].bitcast(I32), 0)
+        nc.vector.memset(w3_sc[:].bitcast(I32), 0)
+        nc.vector.memset(w2_sc[:].bitcast(I32), 0)
+        nc.gpsimd.memset(x_scales[:], 0)
+        make_identity(nc, ident[:])
+
+        def load_words(name, words, first, last):
+            tile = keep.tile([P, last - first, words.shape[3]], U8, name=f"{name}_{first}", align_bytes=64)
+            nc.sync.dma_start(
+                out=tile[:].bitcast(I32),
+                in_=words[first:last].bitcast(I32).rearrange("e s p w -> p (e s) w"),
+            )
+            return {e: tile[:, e - first, :] for e in range(first, last)}
+
+        def load_scales(tile, scales):
+            rows = scales.bitcast(I32).rearrange("e s (q r) w -> r q (e s) w", r=4)
+            for r in range(4):
+                nc.sync.dma_start(out=tile[:].bitcast(I32)[r:P:32], in_=rows[r])
+
+        w1, w3, w2 = {}, {}, {}
+        load_scales(w1_sc, w1_scales)
+        w1.update(load_words("w1", w1_words, 0, 2))
+        w1.update(load_words("w1", w1_words, 2, 5))
+        w3.update(load_words("w3", w3_words, 0, 4))
+        load_scales(w3_sc, w3_scales)
+        w1.update(load_words("w1", w1_words, 5, 8))
+        load_scales(w2_sc, w2_scales)
+        w3.update(load_words("w3", w3_words, 4, 8))
+        w2.update(load_words("w2", w2_words, 0, 4))
+        w2.update(load_words("w2", w2_words, 4, 8))
+
+        for c in range(T // X_CHUNK):
+            lo, mid, hi = c * X_CHUNK, c * X_CHUNK + VECTOR_TOKENS, (c + 1) * X_CHUNK
+            nc.scalar.copy(
+                out=x_grouped[:, mid:hi, :],
+                in_=x_raw[c][:, :, VECTOR_TOKENS:].rearrange("p j w -> p w j"),
+            )
+            nc.vector.tensor_copy(
+                out=x_grouped[:, lo:mid, :],
+                in_=x_raw[c][:, :, :VECTOR_TOKENS].rearrange("p j w -> p w j"),
+            )
+            nc.vector.quantize_mx(
+                out=x_codes[:, lo:hi].bitcast(FP8X4),
+                scales=x_scales[:, lo:hi],
+                in_=x_grouped[:, lo:hi, :].rearrange("p w j -> p (w j)"),
+            )
+
+        a_bank, b_bank, sig_tile, h_tile, y_bank = {}, {}, {}, {}, {}
+
+        def project(e, name, w, sc):
+            cols = slice(e * C, (e + 1) * C)
+            bank = psum.tile([P, H], F32, name=name)
+            nc.tensor.matmul_mx(
+                out=bank[:],
+                lhsT=s_codes[:, cols].bitcast(FP8X4),
+                lhsT_scale=s_scales[:, cols],
+                rhs=w[e].bitcast(FP4X4),
+                rhs_scale=sc[:, e, :],
+                start=True,
+                stop=True,
+            )
+            return bank
+
+        def front(e):
+            cols = slice(e * C, (e + 1) * C)
+            entries = offsets[:, e * C // 16 : (e + 1) * C // 16]
+            nc.vector.tensor_copy(out=s_codes[:, cols], in_=x_codes[:].indirect(entries))
+            nc.vector.tensor_copy(out=s_scales[:, cols], in_=x_scales[:].indirect(entries))
+            a = project(e, "a", w1, w1_sc)
+            sig_tile[e] = sigs.tile([P, 2, P, 2], F32, name="sig")
+            nc.scalar.activation(sig_tile[e][:], a[:].rearrange("p (q u d) -> p u q d", u=2, d=2), SIGMOID)
+
+        def linear(e):
+            if e not in b_bank:
+                b_bank[e] = project(e, "b", w3, w3_sc)
+
+        def gate(e, pieces):
+            h = work.tile([P, 2, P, 2], BF16, name="h")
+            b = b_bank[e][:].rearrange("p (q u d) -> p u q d", u=2, d=2)
+            for u in range(0, 2, 2 // pieces):
+                part = slice(u, u + 2 // pieces)
+                nc.vector.tensor_tensor(h[:, part], b[:, part], sig_tile[e][:, part], MULT)
+            h_tile[e] = h
+
+        def turn(group):
+            bank = psum.tile([P, len(group), 2, P], F32, name="turn")
+            for i, e in enumerate(group):
+                words = h_tile[e][:].rearrange("p u q d -> p (u q d)").bitcast(F32)
+                for u in range(2):
+                    nc.tensor.transpose(bank[:, i, u, :], words[:, u * P : (u + 1) * P], ident[:])
+            return bank
+
+        def second_layer(group, bank, last):
+            n = len(group)
+            hT = work.tile([P, n * C * PACK], BF16, name="hT", align_bytes=64)
+            dst = hT[:].bitcast(F32).rearrange("p (g c u) -> p g c u", g=n, u=2)
+            src = bank[:].rearrange("p g u c -> p g c u")
+            if last:
+                nc.vector.tensor_copy(out=dst, in_=src)
+            else:
+                nc.scalar.copy(out=dst, in_=src)
+            codes = work.tile([P, n * C], U32, name="h_codes", align_bytes=64)
+            scales = work.tile([P, n * C], U8, name="h_scales", align_bytes=64)
+            nc.vector.quantize_mx(out=codes[:].bitcast(FP8X4), scales=scales[:], in_=hT[:])
+            for i, e in enumerate(group):
+                y_bank[e] = []
+                for tiles in ((0, 1), (2,)) if e == E - 1 else ((0, 1, 2),):
+                    y = psum.tile([P, len(tiles), C], F32, name="y")
+                    for j, m in enumerate(tiles):
+                        nc.tensor.matmul_mx(
+                            out=y[:, j, :],
+                            lhsT=w2[e][:, 2 * P * m : 2 * P * (m + 1)].bitcast(FP4X4),
+                            lhsT_scale=w2_sc[:, e, P * m : P * (m + 1)],
+                            rhs=codes[:, i * C : (i + 1) * C].bitcast(FP8X4),
+                            rhs_scale=scales[:, i * C : (i + 1) * C],
+                            start=True,
+                            stop=True,
+                        )
+                    y_bank[e].append((tiles, y))
+
+        width = C // R
+        STORES = [(0, 1, 2, 3), (4, 5), (6,)]
+        staged = {}
+
+        def finish(e):
+            for tiles, bank in y_bank[e]:
+                y = bank[:].rearrange("p m (r u) -> p m r u", r=R)
+                if e == E - 1:
+                    part = keep.tile([P, len(tiles), R, width], F32, name=f"part{tiles[0]}")
+                    if len(tiles) == 1:
+                        nc.vector.tensor_copy(out=part[:], in_=y)
+                    else:
+                        nc.scalar.copy(out=part[:], in_=y)
+                    for j, m in enumerate(tiles):
+                        nc.sync.dma_start(
+                            out=out[m * P : (m + 1) * P, :]
+                            .rearrange("p (r s) -> p r s", r=R)[:, :, e * width : (e + 1) * width],
+                            in_=part[:, j],
+                        )
+                    continue
+                store = [s for s in STORES if e in s][0]
+                if e == store[0]:
+                    staged[store] = keep.tile([P, N_TILES, R, len(store), width], F32, name=f"staged{e}")
+                nc.scalar.copy(out=staged[store][:, :, :, e - store[0], :], in_=y)
+                if e == store[-1]:
+                    for r in range(R):
+                        lo = r * (SLOTS // R) + store[0] * width
+                        nc.sync.dma_start(
+                            out=out[:, lo : lo + len(store) * width].rearrange("(m p) w -> p m w", p=P),
+                            in_=staged[store][:, :, r, :, :].rearrange("p m g u -> p m (g u)"),
+                        )
+
+        GROUPS = [(0, 1), (2, 3), (4, 5), (6,), (7,)]
+        AHEAD = 6
+        LATE = 2
+        for e in range(AHEAD):
+            front(e)
+        upcoming = AHEAD
+        for i in range(len(GROUPS) + LATE):
+            if i < len(GROUPS):
+                group = GROUPS[i]
+                for e in group:
+                    linear(e)
+                for e in group:
+                    gate(e, 2 if e == E - 1 else 1)
+                for e in GROUPS[i + 1] if i + 1 < len(GROUPS) else ():
+                    linear(e)
+                second_layer(group, turn(group), group[-1] == E - 1)
+                for e in group:
+                    if upcoming < E:
+                        front(upcoming)
+                        upcoming += 1
+            if i >= LATE:
+                for e in GROUPS[i - LATE]:
+                    finish(e)

@@ -9,6 +9,7 @@ K, T, E, C, H, N = 512, 512, 8, 128, 512, 384
 R = 2
 SLOTS = E * C
 N_TILES = N // P
+WIDTH = C // R
 FLOPS = 2 * SLOTS * (2 * K * H + H * N)
 
 F32 = mybir.dt.float32
@@ -24,6 +25,8 @@ SIGMOID = mybir.ActivationFunctionType.Sigmoid
 
 X_CHUNK = 256
 VECTOR_TOKENS = 176
+GATHERS = [(0, 1), (1, 2), (2, 4), (4, 6), (6, 8)]
+GROUPS = [(0, 1), (2, 3), (4, 5), (6,), (7,)]
 
 
 def tile_moe_eps_glu_sigmoid_kernel(
@@ -32,9 +35,7 @@ def tile_moe_eps_glu_sigmoid_kernel(
     nc = tc.nc
     with ExitStack() as ctx:
         keep = ctx.enter_context(tc.tile_pool(name="keep", bufs=1))
-        work = ctx.enter_context(tc.tile_pool(name="work", bufs=3))
-        sigs = ctx.enter_context(tc.tile_pool(name="sigs", bufs=8))
-        psum = ctx.enter_context(tc.psum_pool(name="psum", bufs=2))
+        psum = ctx.enter_context(tc.psum_pool(name="psum", bufs=1))
 
         offsets = keep.tile([P, SLOTS // 16], U16, name="offsets")
         x_raw = [keep.tile([P, PACK, X_CHUNK], F32, name=f"x_raw{c}") for c in range(T // X_CHUNK)]
@@ -49,29 +50,30 @@ def tile_moe_eps_glu_sigmoid_kernel(
         ident = keep.tile([P, P], F32, name="ident")
         warm = keep.tile([P, 8], F32, name="warm")
         warm_out = keep.tile([P, 8], F32, name="warm_out")
+        banks = [psum.tile([P, H], F32, name=f"bank{b}") for b in range(8)]
 
-        nc.sync.dma_start(offsets[:], offs)
         for c in range(T // X_CHUNK):
             nc.sync.dma_start(
                 out=x_raw[c][:],
                 in_=xT[:, c * X_CHUNK : (c + 1) * X_CHUNK].rearrange("(p j) w -> p j w", j=PACK),
             )
+        nc.sync.dma_start(offsets[:], offs)
 
         nc.vector.memset(warm[:], 0.0)
         nc.scalar.activation(warm_out[:], warm[:], SIGMOID)
         nc.vector.memset(w1_sc[:].bitcast(I32), 0)
+        nc.vector.memset(x_scales[:].bitcast(I32), 0)
         nc.vector.memset(w3_sc[:].bitcast(I32), 0)
         nc.vector.memset(w2_sc[:].bitcast(I32), 0)
-        nc.gpsimd.memset(x_scales[:], 0)
         make_identity(nc, ident[:])
 
-        def load_words(name, words, first, last):
+        def load_words(table, name, words, first, last):
             tile = keep.tile([P, last - first, words.shape[3]], U8, name=f"{name}_{first}", align_bytes=64)
             nc.sync.dma_start(
                 out=tile[:].bitcast(I32),
                 in_=words[first:last].bitcast(I32).rearrange("e s p w -> p (e s) w"),
             )
-            return {e: tile[:, e - first, :] for e in range(first, last)}
+            table.update({e: tile[:, e - first, :] for e in range(first, last)})
 
         def load_scales(tile, scales):
             rows = scales.bitcast(I32).rearrange("e s (q r) w -> r q (e s) w", r=4)
@@ -80,15 +82,18 @@ def tile_moe_eps_glu_sigmoid_kernel(
 
         w1, w3, w2 = {}, {}, {}
         load_scales(w1_sc, w1_scales)
-        w1.update(load_words("w1", w1_words, 0, 2))
-        w1.update(load_words("w1", w1_words, 2, 5))
-        w3.update(load_words("w3", w3_words, 0, 4))
+        load_words(w1, "w1", w1_words, 0, 2)
+        load_words(w1, "w1", w1_words, 2, 6)
         load_scales(w3_sc, w3_scales)
-        w1.update(load_words("w1", w1_words, 5, 8))
         load_scales(w2_sc, w2_scales)
-        w3.update(load_words("w3", w3_words, 4, 8))
-        w2.update(load_words("w2", w2_words, 0, 4))
-        w2.update(load_words("w2", w2_words, 4, 8))
+        load_words(w3, "w3", w3_words, 0, 2)
+        load_words(w1, "w1", w1_words, 6, 8)
+        load_words(w3, "w3", w3_words, 2, 4)
+        load_words(w3, "w3", w3_words, 4, 6)
+        load_words(w2, "w2", w2_words, 0, 2)
+        load_words(w3, "w3", w3_words, 6, 8)
+        load_words(w2, "w2", w2_words, 2, 4)
+        load_words(w2, "w2", w2_words, 4, 8)
 
         for c in range(T // X_CHUNK):
             lo, mid, hi = c * X_CHUNK, c * X_CHUNK + VECTOR_TOKENS, (c + 1) * X_CHUNK
@@ -106,11 +111,16 @@ def tile_moe_eps_glu_sigmoid_kernel(
                 in_=x_grouped[:, lo:hi, :].rearrange("p w j -> p (w j)"),
             )
 
-        a_bank, b_bank, sig_tile, h_tile, y_bank = {}, {}, {}, {}, {}
+        for first, last in GATHERS:
+            cols = slice(first * C, last * C)
+            entries = offsets[:, first * C // 16 : last * C // 16]
+            nc.vector.tensor_copy(out=s_codes[:, cols], in_=x_codes[:].indirect(entries))
+            nc.vector.tensor_copy(out=s_scales[:, cols], in_=x_scales[:].indirect(entries))
 
-        def project(e, name, w, sc):
+        sig, h, hT, codes, scales, staged = {}, {}, {}, {}, {}, {}
+
+        def project(e, bank, w, sc):
             cols = slice(e * C, (e + 1) * C)
-            bank = psum.tile([P, H], F32, name=name)
             nc.tensor.matmul_mx(
                 out=bank[:],
                 lhsT=s_codes[:, cols].bitcast(FP8X4),
@@ -120,117 +130,107 @@ def tile_moe_eps_glu_sigmoid_kernel(
                 start=True,
                 stop=True,
             )
-            return bank
 
-        def front(e):
-            cols = slice(e * C, (e + 1) * C)
-            entries = offsets[:, e * C // 16 : (e + 1) * C // 16]
-            nc.vector.tensor_copy(out=s_codes[:, cols], in_=x_codes[:].indirect(entries))
-            nc.vector.tensor_copy(out=s_scales[:, cols], in_=x_scales[:].indirect(entries))
-            a = project(e, "a", w1, w1_sc)
-            sig_tile[e] = sigs.tile([P, 2, P, 2], F32, name="sig")
-            nc.scalar.activation(sig_tile[e][:], a[:].rearrange("p (q u d) -> p u q d", u=2, d=2), SIGMOID)
+        def a_step(e):
+            bank = banks[e % 2]
+            project(e, bank, w1, w1_sc)
+            sig[e] = keep.tile([P, 2, P, 2], F32, name=f"sig{e}")
+            nc.scalar.activation(sig[e][:], bank[:].rearrange("p (q u d) -> p u q d", u=2, d=2), SIGMOID)
 
-        def linear(e):
-            if e not in b_bank:
-                b_bank[e] = project(e, "b", w3, w3_sc)
+        def b_step(e):
+            project(e, banks[2 + e % 4], w3, w3_sc)
 
-        def gate(e, pieces):
-            h = work.tile([P, 2, P, 2], BF16, name="h")
-            b = b_bank[e][:].rearrange("p (q u d) -> p u q d", u=2, d=2)
-            for u in range(0, 2, 2 // pieces):
-                part = slice(u, u + 2 // pieces)
-                nc.vector.tensor_tensor(h[:, part], b[:, part], sig_tile[e][:, part], MULT)
-            h_tile[e] = h
-
-        def turn(group):
-            bank = psum.tile([P, len(group), 2, P], F32, name="turn")
+        def gate(g, pieces=1):
+            group = GROUPS[g]
+            h[g] = keep.tile([P, len(group), 2, P, 2], BF16, name=f"h{g}")
             for i, e in enumerate(group):
-                words = h_tile[e][:].rearrange("p u q d -> p (u q d)").bitcast(F32)
-                for u in range(2):
-                    nc.tensor.transpose(bank[:, i, u, :], words[:, u * P : (u + 1) * P], ident[:])
-            return bank
+                b = banks[2 + e % 4][:].rearrange("p (q u d) -> p u q d", u=2, d=2)
+                for u in range(0, 2, 2 // pieces):
+                    part = slice(u, u + 2 // pieces)
+                    nc.vector.tensor_tensor(h[g][:, i, part], b[:, part], sig[e][:, part], MULT)
 
-        def second_layer(group, bank, last):
+        def turn(g, engine):
+            n = len(GROUPS[g])
+            bank = banks[6 + g % 2][:, : n * 2 * P].rearrange("p (g u c) -> p g u c", g=n, u=2)
+            words = h[g][:].rearrange("p g u q d -> p (g u q d)").bitcast(F32)
+            for j in range(2 * n):
+                nc.tensor.transpose(bank[:, j // 2, j % 2, :], words[:, j * P : (j + 1) * P], ident[:])
+            hT[g] = keep.tile([P, n * C * PACK], BF16, name=f"hT{g}", align_bytes=64)
+            dst = hT[g][:].bitcast(F32).rearrange("p (g c u) -> p g c u", g=n, u=2)
+            engine(out=dst, in_=bank.rearrange("p g u c -> p g c u"))
+
+        def y_places(e):
+            if e == E - 1:
+                return [(banks[5], 0, 2), (banks[2], 2, 1)]
+            return [(banks[(0, 1, 2, 3, 0, 1, 4)[e]], 0, 3)]
+
+        def second(g):
+            group = GROUPS[g]
             n = len(group)
-            hT = work.tile([P, n * C * PACK], BF16, name="hT", align_bytes=64)
-            dst = hT[:].bitcast(F32).rearrange("p (g c u) -> p g c u", g=n, u=2)
-            src = bank[:].rearrange("p g u c -> p g c u")
-            if last:
-                nc.vector.tensor_copy(out=dst, in_=src)
-            else:
-                nc.scalar.copy(out=dst, in_=src)
-            codes = work.tile([P, n * C], U32, name="h_codes", align_bytes=64)
-            scales = work.tile([P, n * C], U8, name="h_scales", align_bytes=64)
-            nc.vector.quantize_mx(out=codes[:].bitcast(FP8X4), scales=scales[:], in_=hT[:])
+            codes[g] = keep.tile([P, n * C], U32, name=f"h_codes{g}", align_bytes=64)
+            scales[g] = keep.tile([P, n * C], U8, name=f"h_scales{g}", align_bytes=64)
+            nc.vector.quantize_mx(out=codes[g][:].bitcast(FP8X4), scales=scales[g][:], in_=hT[g][:])
             for i, e in enumerate(group):
-                y_bank[e] = []
-                for tiles in ((0, 1), (2,)) if e == E - 1 else ((0, 1, 2),):
-                    y = psum.tile([P, len(tiles), C], F32, name="y")
-                    for j, m in enumerate(tiles):
+                for bank, first, count in y_places(e):
+                    for j in range(count):
+                        m = first + j
                         nc.tensor.matmul_mx(
-                            out=y[:, j, :],
+                            out=bank[:, j * C : (j + 1) * C],
                             lhsT=w2[e][:, 2 * P * m : 2 * P * (m + 1)].bitcast(FP4X4),
                             lhsT_scale=w2_sc[:, e, P * m : P * (m + 1)],
-                            rhs=codes[:, i * C : (i + 1) * C].bitcast(FP8X4),
-                            rhs_scale=scales[:, i * C : (i + 1) * C],
+                            rhs=codes[g][:, i * C : (i + 1) * C].bitcast(FP8X4),
+                            rhs_scale=scales[g][:, i * C : (i + 1) * C],
                             start=True,
                             stop=True,
                         )
-                    y_bank[e].append((tiles, y))
 
-        width = C // R
-        STORES = [(0, 1, 2, 3), (4, 5), (6,)]
-        staged = {}
+        def finish(g, engines):
+            group = GROUPS[g]
+            n = len(group)
+            staged[g] = keep.tile([P, N_TILES, R, n, WIDTH], F32, name=f"staged{g}")
+            places = [(i, place) for i, e in enumerate(group) for place in y_places(e)]
+            for engine, (i, (bank, first, count)) in zip(engines, places):
+                engine(
+                    out=staged[g][:, first : first + count, :, i, :],
+                    in_=bank[:, : count * C].rearrange("p (m r u) -> p m r u", r=R, u=WIDTH),
+                )
+            for r in range(R):
+                lo = r * (SLOTS // R) + group[0] * WIDTH
+                nc.sync.dma_start(
+                    out=out[:, lo : lo + n * WIDTH].rearrange("(m p) w -> p m w", p=P),
+                    in_=staged[g][:, :, r, :, :].rearrange("p m g u -> p m (g u)"),
+                )
 
-        def finish(e):
-            for tiles, bank in y_bank[e]:
-                y = bank[:].rearrange("p m (r u) -> p m r u", r=R)
-                if e == E - 1:
-                    part = keep.tile([P, len(tiles), R, width], F32, name=f"part{tiles[0]}")
-                    if len(tiles) == 1:
-                        nc.vector.tensor_copy(out=part[:], in_=y)
-                    else:
-                        nc.scalar.copy(out=part[:], in_=y)
-                    for j, m in enumerate(tiles):
-                        nc.sync.dma_start(
-                            out=out[m * P : (m + 1) * P, :]
-                            .rearrange("p (r s) -> p r s", r=R)[:, :, e * width : (e + 1) * width],
-                            in_=part[:, j],
-                        )
-                    continue
-                store = [s for s in STORES if e in s][0]
-                if e == store[0]:
-                    staged[store] = keep.tile([P, N_TILES, R, len(store), width], F32, name=f"staged{e}")
-                nc.scalar.copy(out=staged[store][:, :, :, e - store[0], :], in_=y)
-                if e == store[-1]:
-                    for r in range(R):
-                        lo = r * (SLOTS // R) + store[0] * width
-                        nc.sync.dma_start(
-                            out=out[:, lo : lo + len(store) * width].rearrange("(m p) w -> p m w", p=P),
-                            in_=staged[store][:, :, r, :, :].rearrange("p m g u -> p m (g u)"),
-                        )
-
-        GROUPS = [(0, 1), (2, 3), (4, 5), (6,), (7,)]
-        AHEAD = 6
-        LATE = 2
-        for e in range(AHEAD):
-            front(e)
-        upcoming = AHEAD
-        for i in range(len(GROUPS) + LATE):
-            if i < len(GROUPS):
-                group = GROUPS[i]
-                for e in group:
-                    linear(e)
-                for e in group:
-                    gate(e, 2 if e == E - 1 else 1)
-                for e in GROUPS[i + 1] if i + 1 < len(GROUPS) else ():
-                    linear(e)
-                second_layer(group, turn(group), group[-1] == E - 1)
-                for e in group:
-                    if upcoming < E:
-                        front(upcoming)
-                        upcoming += 1
-            if i >= LATE:
-                for e in GROUPS[i - LATE]:
-                    finish(e)
+        scalar, vector = nc.scalar.copy, nc.vector.tensor_copy
+        for e in range(6):
+            a_step(e)
+        b_step(0)
+        b_step(1)
+        a_step(6)
+        a_step(7)
+        b_step(2)
+        b_step(3)
+        gate(0)
+        turn(0, scalar)
+        b_step(4)
+        b_step(5)
+        second(0)
+        gate(1)
+        turn(1, scalar)
+        b_step(6)
+        b_step(7)
+        gate(2)
+        second(1)
+        turn(2, scalar)
+        finish(0, (scalar, scalar))
+        gate(3)
+        turn(3, scalar)
+        second(2)
+        gate(4, 2)
+        turn(4, scalar)
+        second(3)
+        finish(1, (scalar, scalar))
+        second(4)
+        finish(2, (scalar, vector))
+        finish(3, (scalar,))
+        finish(4, (scalar, vector))

@@ -23,10 +23,10 @@ FP4X4 = mybir.dt.float4_e2m1fn_x4
 MULT = mybir.AluOpType.mult
 SIGMOID = mybir.ActivationFunctionType.Sigmoid
 
-X_CHUNK = 256
-VECTOR_TOKENS = 176
+X_CHUNKS = [(0, 160, 256), (256, 344, 384), (384, 472, 512)]
 GATHERS = [(0, 1), (1, 2), (2, 4), (4, 6), (6, 8)]
 GROUPS = [(0, 1), (2, 3), (4, 5), (6,), (7,)]
+STORES = [(0, 1), (2, 3), (4, 5), (6, 7)]
 
 
 def tile_moe_eps_glu_sigmoid_kernel(
@@ -38,7 +38,7 @@ def tile_moe_eps_glu_sigmoid_kernel(
         psum = ctx.enter_context(tc.psum_pool(name="psum", bufs=1))
 
         offsets = keep.tile([P, SLOTS // 16], U16, name="offsets")
-        x_raw = [keep.tile([P, PACK, X_CHUNK], F32, name=f"x_raw{c}") for c in range(T // X_CHUNK)]
+        x_raw = [keep.tile([P, PACK, hi - lo], F32, name=f"x_raw{lo}") for lo, mid, hi in X_CHUNKS]
         x_grouped = keep.tile([P, T, PACK], BF16, name="x_grouped", align_bytes=64)
         x_codes = keep.tile([P, T], U32, name="x_codes", align_bytes=64)
         x_scales = keep.tile([P, T], U8, name="x_scales", align_bytes=64)
@@ -52,11 +52,8 @@ def tile_moe_eps_glu_sigmoid_kernel(
         warm_out = keep.tile([P, 8], F32, name="warm_out")
         banks = [psum.tile([P, H], F32, name=f"bank{b}") for b in range(8)]
 
-        for c in range(T // X_CHUNK):
-            nc.sync.dma_start(
-                out=x_raw[c][:],
-                in_=xT[:, c * X_CHUNK : (c + 1) * X_CHUNK].rearrange("(p j) w -> p j w", j=PACK),
-            )
+        for raw, (lo, mid, hi) in zip(x_raw, X_CHUNKS):
+            nc.sync.dma_start(out=raw[:], in_=xT[:, lo:hi].rearrange("(p j) w -> p j w", j=PACK))
         nc.sync.dma_start(offsets[:], offs)
 
         nc.vector.memset(warm[:], 0.0)
@@ -95,15 +92,14 @@ def tile_moe_eps_glu_sigmoid_kernel(
         load_words(w2, "w2", w2_words, 2, 4)
         load_words(w2, "w2", w2_words, 4, 8)
 
-        for c in range(T // X_CHUNK):
-            lo, mid, hi = c * X_CHUNK, c * X_CHUNK + VECTOR_TOKENS, (c + 1) * X_CHUNK
+        for raw, (lo, mid, hi) in zip(x_raw, X_CHUNKS):
             nc.scalar.copy(
                 out=x_grouped[:, mid:hi, :],
-                in_=x_raw[c][:, :, VECTOR_TOKENS:].rearrange("p j w -> p w j"),
+                in_=raw[:, :, mid - lo :].rearrange("p j w -> p w j"),
             )
             nc.vector.tensor_copy(
                 out=x_grouped[:, lo:mid, :],
-                in_=x_raw[c][:, :, :VECTOR_TOKENS].rearrange("p j w -> p w j"),
+                in_=raw[:, :, : mid - lo].rearrange("p j w -> p w j"),
             )
             nc.vector.quantize_mx(
                 out=x_codes[:, lo:hi].bitcast(FP8X4),
@@ -132,7 +128,7 @@ def tile_moe_eps_glu_sigmoid_kernel(
             )
 
         def a_step(e):
-            bank = banks[e % 2]
+            bank = banks[(6, 7, 0, 1)[e % 4]]
             project(e, bank, w1, w1_sc)
             sig[e] = keep.tile([P, 2, P, 2], F32, name=f"sig{e}")
             nc.scalar.activation(sig[e][:], bank[:].rearrange("p (q u d) -> p u q d", u=2, d=2), SIGMOID)
@@ -184,22 +180,23 @@ def tile_moe_eps_glu_sigmoid_kernel(
                             stop=True,
                         )
 
-        def finish(g, engines):
-            group = GROUPS[g]
-            n = len(group)
-            staged[g] = keep.tile([P, N_TILES, R, n, WIDTH], F32, name=f"staged{g}")
-            places = [(i, place) for i, e in enumerate(group) for place in y_places(e)]
-            for engine, (i, (bank, first, count)) in zip(engines, places):
+        def finish(e, *engines):
+            store = [s for s in STORES if e in s][0]
+            n = len(store)
+            if e == store[0]:
+                staged[store] = keep.tile([P, N_TILES, R, n, WIDTH], F32, name=f"staged{e}")
+            for engine, (bank, first, count) in zip(engines, y_places(e)):
                 engine(
-                    out=staged[g][:, first : first + count, :, i, :],
+                    out=staged[store][:, first : first + count, :, e - store[0], :],
                     in_=bank[:, : count * C].rearrange("p (m r u) -> p m r u", r=R, u=WIDTH),
                 )
-            for r in range(R):
-                lo = r * (SLOTS // R) + group[0] * WIDTH
-                nc.sync.dma_start(
-                    out=out[:, lo : lo + n * WIDTH].rearrange("(m p) w -> p m w", p=P),
-                    in_=staged[g][:, :, r, :, :].rearrange("p m g u -> p m (g u)"),
-                )
+            if e == store[-1]:
+                for r in range(R):
+                    lo = r * (SLOTS // R) + store[0] * WIDTH
+                    nc.sync.dma_start(
+                        out=out[:, lo : lo + n * WIDTH].rearrange("(m p) w -> p m w", p=P),
+                        in_=staged[store][:, :, r, :, :].rearrange("p m g u -> p m (g u)"),
+                    )
 
         scalar, vector = nc.scalar.copy, nc.vector.tensor_copy
         for e in range(6):
@@ -222,15 +219,18 @@ def tile_moe_eps_glu_sigmoid_kernel(
         gate(2)
         second(1)
         turn(2, scalar)
-        finish(0, (scalar, scalar))
+        finish(0, scalar)
+        finish(1, scalar)
         gate(3)
-        turn(3, scalar)
+        turn(3, vector)
         second(2)
         gate(4, 2)
-        turn(4, scalar)
+        turn(4, vector)
         second(3)
-        finish(1, (scalar, scalar))
+        finish(2, scalar)
+        finish(3, scalar)
         second(4)
-        finish(2, (scalar, vector))
-        finish(3, (scalar,))
-        finish(4, (scalar, vector))
+        finish(4, scalar)
+        finish(5, vector)
+        finish(6, scalar)
+        finish(7, scalar, vector)

@@ -24,7 +24,8 @@ MULT = mybir.AluOpType.mult
 SIGMOID = mybir.ActivationFunctionType.Sigmoid
 
 X_CHUNKS = [(0, 160, 256), (256, 344, 384), (384, 472, 512)]
-GATHERS = [(0, 1), (1, 2), (2, 4), (4, 6), (6, 8)]
+HELD = 6
+B_BANKS = (2, 3, 2, 3, 4, 2, 3, 0)
 GROUPS = [(0, 1), (2, 3), (4, 5), (6,), (7,)]
 STORES = [(0, 1), (2, 3), (4, 5), (6, 7)]
 
@@ -42,22 +43,18 @@ def tile_moe_eps_glu_sigmoid_kernel(
         x_grouped = keep.tile([P, T, PACK], BF16, name="x_grouped", align_bytes=64)
         x_codes = keep.tile([P, T], U32, name="x_codes", align_bytes=64)
         x_scales = keep.tile([P, T], U8, name="x_scales", align_bytes=64)
-        s_codes = keep.tile([P, SLOTS], U32, name="s_codes", align_bytes=64)
-        s_scales = keep.tile([P, SLOTS], U8, name="s_scales", align_bytes=64)
+        s_codes = keep.tile([P, HELD * C], U32, name="s_codes", align_bytes=64)
+        s_scales = keep.tile([P, HELD * C], U8, name="s_scales", align_bytes=64)
         w1_sc = keep.tile([P, E, H], U8, name="w1_sc", align_bytes=64)
         w3_sc = keep.tile([P, E, H], U8, name="w3_sc", align_bytes=64)
         w2_sc = keep.tile([P, E, N], U8, name="w2_sc", align_bytes=64)
         ident = keep.tile([P, P], F32, name="ident")
-        warm = keep.tile([P, 8], F32, name="warm")
-        warm_out = keep.tile([P, 8], F32, name="warm_out")
         banks = [psum.tile([P, H], F32, name=f"bank{b}") for b in range(8)]
 
         for raw, (lo, mid, hi) in zip(x_raw, X_CHUNKS):
             nc.sync.dma_start(out=raw[:], in_=xT[:, lo:hi].rearrange("(p j) w -> p j w", j=PACK))
         nc.sync.dma_start(offsets[:], offs)
 
-        nc.vector.memset(warm[:], 0.0)
-        nc.scalar.activation(warm_out[:], warm[:], SIGMOID)
         nc.vector.memset(w1_sc[:].bitcast(I32), 0)
         nc.vector.memset(x_scales[:].bitcast(I32), 0)
         nc.vector.memset(w3_sc[:].bitcast(I32), 0)
@@ -80,17 +77,19 @@ def tile_moe_eps_glu_sigmoid_kernel(
         w1, w3, w2 = {}, {}, {}
         load_scales(w1_sc, w1_scales)
         load_words(w1, "w1", w1_words, 0, 2)
-        load_words(w1, "w1", w1_words, 2, 6)
         load_scales(w3_sc, w3_scales)
-        load_scales(w2_sc, w2_scales)
         load_words(w3, "w3", w3_words, 0, 2)
-        load_words(w1, "w1", w1_words, 6, 8)
+        load_words(w1, "w1", w1_words, 2, 4)
+        load_scales(w2_sc, w2_scales)
+        load_words(w1, "w1", w1_words, 4, 6)
         load_words(w3, "w3", w3_words, 2, 4)
+        load_words(w1, "w1", w1_words, 6, 8)
         load_words(w3, "w3", w3_words, 4, 6)
         load_words(w2, "w2", w2_words, 0, 2)
         load_words(w3, "w3", w3_words, 6, 8)
         load_words(w2, "w2", w2_words, 2, 4)
-        load_words(w2, "w2", w2_words, 4, 8)
+        load_words(w2, "w2", w2_words, 4, 6)
+        load_words(w2, "w2", w2_words, 6, 8)
 
         for raw, (lo, mid, hi) in zip(x_raw, X_CHUNKS):
             nc.scalar.copy(
@@ -107,8 +106,8 @@ def tile_moe_eps_glu_sigmoid_kernel(
                 in_=x_grouped[:, lo:hi, :].rearrange("p w j -> p (w j)"),
             )
 
-        for first, last in GATHERS:
-            cols = slice(first * C, last * C)
+        def gather(first, last):
+            cols = slice(first % HELD * C, (first % HELD + last - first) * C)
             entries = offsets[:, first * C // 16 : last * C // 16]
             nc.vector.tensor_copy(out=s_codes[:, cols], in_=x_codes[:].indirect(entries))
             nc.vector.tensor_copy(out=s_scales[:, cols], in_=x_scales[:].indirect(entries))
@@ -116,7 +115,7 @@ def tile_moe_eps_glu_sigmoid_kernel(
         sig, h, hT, codes, scales, staged = {}, {}, {}, {}, {}, {}
 
         def project(e, bank, w, sc):
-            cols = slice(e * C, (e + 1) * C)
+            cols = slice(e % HELD * C, (e % HELD + 1) * C)
             nc.tensor.matmul_mx(
                 out=bank[:],
                 lhsT=s_codes[:, cols].bitcast(FP8X4),
@@ -128,26 +127,26 @@ def tile_moe_eps_glu_sigmoid_kernel(
             )
 
         def a_step(e):
-            bank = banks[(6, 7, 0, 1)[e % 4]]
+            bank = banks[(6, 7, 0, 1, 6, 7, 0, 1)[e]]
             project(e, bank, w1, w1_sc)
             sig[e] = keep.tile([P, 2, P, 2], F32, name=f"sig{e}")
             nc.scalar.activation(sig[e][:], bank[:].rearrange("p (q u d) -> p u q d", u=2, d=2), SIGMOID)
 
         def b_step(e):
-            project(e, banks[2 + e % 4], w3, w3_sc)
+            project(e, banks[B_BANKS[e]], w3, w3_sc)
 
-        def gate(g, pieces=1):
-            group = GROUPS[g]
-            h[g] = keep.tile([P, len(group), 2, P, 2], BF16, name=f"h{g}")
-            for i, e in enumerate(group):
-                b = banks[2 + e % 4][:].rearrange("p (q u d) -> p u q d", u=2, d=2)
-                for u in range(0, 2, 2 // pieces):
-                    part = slice(u, u + 2 // pieces)
-                    nc.vector.tensor_tensor(h[g][:, i, part], b[:, part], sig[e][:, part], MULT)
+        def gate(e, pieces=1):
+            g, i = [(g, group.index(e)) for g, group in enumerate(GROUPS) if e in group][0]
+            if i == 0:
+                h[g] = keep.tile([P, len(GROUPS[g]), 2, P, 2], BF16, name=f"h{g}")
+            b = banks[B_BANKS[e]][:].rearrange("p (q u d) -> p u q d", u=2, d=2)
+            for u in range(0, 2, 2 // pieces):
+                part = slice(u, u + 2 // pieces)
+                nc.vector.tensor_tensor(h[g][:, i, part], b[:, part], sig[e][:, part], MULT)
 
         def turn(g, engine):
             n = len(GROUPS[g])
-            bank = banks[6 + g % 2][:, : n * 2 * P].rearrange("p (g u c) -> p g u c", g=n, u=2)
+            bank = banks[(4, 5, 1, 4, 2)[g]][:, : n * 2 * P].rearrange("p (g u c) -> p g u c", g=n, u=2)
             words = h[g][:].rearrange("p g u q d -> p (g u q d)").bitcast(F32)
             for j in range(2 * n):
                 nc.tensor.transpose(bank[:, j // 2, j % 2, :], words[:, j * P : (j + 1) * P], ident[:])
@@ -157,28 +156,29 @@ def tile_moe_eps_glu_sigmoid_kernel(
 
         def y_places(e):
             if e == E - 1:
-                return [(banks[5], 0, 2), (banks[2], 2, 1)]
-            return [(banks[(0, 1, 2, 3, 0, 1, 4)[e]], 0, 3)]
+                return [(banks[0], 0, 2), (banks[5], 2, 1)]
+            return [(banks[(6, 7, 5, 6, 7, 1, 3)[e]], 0, 3)]
 
-        def second(g):
-            group = GROUPS[g]
-            n = len(group)
+        def quantise(g):
+            n = len(GROUPS[g])
             codes[g] = keep.tile([P, n * C], U32, name=f"h_codes{g}", align_bytes=64)
             scales[g] = keep.tile([P, n * C], U8, name=f"h_scales{g}", align_bytes=64)
             nc.vector.quantize_mx(out=codes[g][:].bitcast(FP8X4), scales=scales[g][:], in_=hT[g][:])
-            for i, e in enumerate(group):
-                for bank, first, count in y_places(e):
-                    for j in range(count):
-                        m = first + j
-                        nc.tensor.matmul_mx(
-                            out=bank[:, j * C : (j + 1) * C],
-                            lhsT=w2[e][:, 2 * P * m : 2 * P * (m + 1)].bitcast(FP4X4),
-                            lhsT_scale=w2_sc[:, e, P * m : P * (m + 1)],
-                            rhs=codes[g][:, i * C : (i + 1) * C].bitcast(FP8X4),
-                            rhs_scale=scales[g][:, i * C : (i + 1) * C],
-                            start=True,
-                            stop=True,
-                        )
+
+        def y_step(e):
+            g, i = [(g, group.index(e)) for g, group in enumerate(GROUPS) if e in group][0]
+            for bank, first, count in y_places(e):
+                for j in range(count):
+                    m = first + j
+                    nc.tensor.matmul_mx(
+                        out=bank[:, j * C : (j + 1) * C],
+                        lhsT=w2[e][:, 2 * P * m : 2 * P * (m + 1)].bitcast(FP4X4),
+                        lhsT_scale=w2_sc[:, e, P * m : P * (m + 1)],
+                        rhs=codes[g][:, i * C : (i + 1) * C].bitcast(FP8X4),
+                        rhs_scale=scales[g][:, i * C : (i + 1) * C],
+                        start=True,
+                        stop=True,
+                    )
 
         def finish(e, *engines):
             store = [s for s in STORES if e in s][0]
@@ -199,37 +199,57 @@ def tile_moe_eps_glu_sigmoid_kernel(
                     )
 
         scalar, vector = nc.scalar.copy, nc.vector.tensor_copy
-        for e in range(6):
-            a_step(e)
+        gather(0, 1)
+        gather(1, 2)
+        gather(2, 4)
+        gather(4, 6)
+        a_step(0)
+        a_step(1)
         b_step(0)
         b_step(1)
-        a_step(6)
-        a_step(7)
+        a_step(2)
+        a_step(3)
+        gate(0)
+        gate(1)
+        turn(0, scalar)
+        gather(6, 8)
+        a_step(4)
+        a_step(5)
         b_step(2)
         b_step(3)
-        gate(0)
-        turn(0, scalar)
+        a_step(6)
+        a_step(7)
         b_step(4)
+        quantise(0)
+        gate(2)
         b_step(5)
-        second(0)
-        gate(1)
+        gate(3)
         turn(1, scalar)
+        y_step(0)
+        y_step(1)
         b_step(6)
         b_step(7)
-        gate(2)
-        second(1)
-        turn(2, scalar)
         finish(0, scalar)
         finish(1, scalar)
-        gate(3)
-        turn(3, vector)
-        second(2)
-        gate(4, 2)
-        turn(4, vector)
-        second(3)
+        quantise(1)
+        y_step(2)
+        y_step(3)
+        gate(4)
+        gate(5)
+        turn(2, scalar)
         finish(2, scalar)
         finish(3, scalar)
-        second(4)
+        gate(6)
+        turn(3, vector)
+        quantise(2)
+        y_step(4)
+        y_step(5)
+        gate(7, 2)
+        turn(4, vector)
+        quantise(3)
+        y_step(6)
+        quantise(4)
+        y_step(7)
         finish(4, scalar)
         finish(5, vector)
         finish(6, scalar)

@@ -10,6 +10,7 @@ R = 2
 SLOTS = E * C
 N_TILES = N // P
 WIDTH = C // R
+BANKS = 8
 FLOPS = 2 * SLOTS * (2 * K * H + H * N)
 
 F32 = mybir.dt.float32
@@ -23,11 +24,11 @@ FP4X4 = mybir.dt.float4_e2m1fn_x4
 MULT = mybir.AluOpType.mult
 SIGMOID = mybir.ActivationFunctionType.Sigmoid
 
-X_CHUNKS = [(0, 160, 256), (256, 344, 384), (384, 472, 512)]
-HELD = 6
-B_BANKS = (2, 3, 2, 3, 4, 2, 3, 0)
+X_LOADS = [(0, 256, 384), (384, 472, 512)]
+X_QUANTISED = [(0, 256), (256, 384), (384, 512)]
+PAIRS = [(0, 1), (2, 3), (4, 5), (6, 7)]
 GROUPS = [(0, 1), (2, 3), (4, 5), (6,), (7,)]
-STORES = [(0, 1), (2, 3), (4, 5), (6, 7)]
+HELD = 6
 
 
 def tile_moe_eps_glu_sigmoid_kernel(
@@ -39,218 +40,207 @@ def tile_moe_eps_glu_sigmoid_kernel(
         psum = ctx.enter_context(tc.psum_pool(name="psum", bufs=1))
 
         offsets = keep.tile([P, SLOTS // 16], U16, name="offsets")
-        x_raw = [keep.tile([P, PACK, hi - lo], F32, name=f"x_raw{lo}") for lo, mid, hi in X_CHUNKS]
+        x_raw = [keep.tile([P, PACK, end - first], F32, name=f"x_raw{first}") for first, split, end in X_LOADS]
         x_grouped = keep.tile([P, T, PACK], BF16, name="x_grouped", align_bytes=64)
         x_codes = keep.tile([P, T], U32, name="x_codes", align_bytes=64)
         x_scales = keep.tile([P, T], U8, name="x_scales", align_bytes=64)
-        s_codes = keep.tile([P, HELD * C], U32, name="s_codes", align_bytes=64)
-        s_scales = keep.tile([P, HELD * C], U8, name="s_scales", align_bytes=64)
+        slot_codes = keep.tile([P, HELD * C], U32, name="slot_codes", align_bytes=64)
+        slot_scales = keep.tile([P, HELD * C], U8, name="slot_scales", align_bytes=64)
         w1_sc = keep.tile([P, E, H], U8, name="w1_sc", align_bytes=64)
         w3_sc = keep.tile([P, E, H], U8, name="w3_sc", align_bytes=64)
         w2_sc = keep.tile([P, E, N], U8, name="w2_sc", align_bytes=64)
         ident = keep.tile([P, P], F32, name="ident")
-        banks = [psum.tile([P, H], F32, name=f"bank{b}") for b in range(8)]
+        free_banks = [psum.tile([P, H], F32, name=f"bank{b}") for b in range(BANKS)]
 
-        for raw, (lo, mid, hi) in zip(x_raw, X_CHUNKS):
-            nc.sync.dma_start(out=raw[:], in_=xT[:, lo:hi].rearrange("(p j) w -> p j w", j=PACK))
+        for raw, (first, split, end) in zip(x_raw, X_LOADS):
+            nc.sync.dma_start(out=raw[:], in_=xT[:, first:end].rearrange("(p j) w -> p j w", j=PACK))
         nc.sync.dma_start(offsets[:], offs)
 
-        nc.vector.memset(w1_sc[:].bitcast(I32), 0)
-        nc.vector.memset(x_scales[:].bitcast(I32), 0)
-        nc.vector.memset(w3_sc[:].bitcast(I32), 0)
-        nc.vector.memset(w2_sc[:].bitcast(I32), 0)
+        for scale_tile in (w1_sc, x_scales, w3_sc, w2_sc):
+            nc.vector.memset(scale_tile[:].bitcast(I32), 0)
         make_identity(nc, ident[:])
 
-        def load_words(table, name, words, first, last):
-            tile = keep.tile([P, last - first, words.shape[3]], U8, name=f"{name}_{first}", align_bytes=64)
+        w1, w3, w2 = {}, {}, {}
+
+        def load_words(table, name, words, pair):
+            tile = keep.tile([P, len(pair), words.shape[3]], U8, name=f"{name}_{pair[0]}", align_bytes=64)
             nc.sync.dma_start(
                 out=tile[:].bitcast(I32),
-                in_=words[first:last].bitcast(I32).rearrange("e s p w -> p (e s) w"),
+                in_=words[pair[0] : pair[-1] + 1].bitcast(I32).rearrange("e s p w -> p (e s) w"),
             )
-            table.update({e: tile[:, e - first, :] for e in range(first, last)})
+            table.update({e: tile[:, i, :] for i, e in enumerate(pair)})
 
         def load_scales(tile, scales):
             rows = scales.bitcast(I32).rearrange("e s (q r) w -> r q (e s) w", r=4)
             for r in range(4):
                 nc.sync.dma_start(out=tile[:].bitcast(I32)[r:P:32], in_=rows[r])
 
-        w1, w3, w2 = {}, {}, {}
         load_scales(w1_sc, w1_scales)
-        load_words(w1, "w1", w1_words, 0, 2)
+        load_words(w1, "w1", w1_words, PAIRS[0])
         load_scales(w3_sc, w3_scales)
-        load_words(w3, "w3", w3_words, 0, 2)
-        load_words(w1, "w1", w1_words, 2, 4)
+        load_words(w3, "w3", w3_words, PAIRS[0])
+        load_words(w1, "w1", w1_words, PAIRS[1])
         load_scales(w2_sc, w2_scales)
-        load_words(w1, "w1", w1_words, 4, 6)
-        load_words(w3, "w3", w3_words, 2, 4)
-        load_words(w1, "w1", w1_words, 6, 8)
-        load_words(w3, "w3", w3_words, 4, 6)
-        load_words(w2, "w2", w2_words, 0, 2)
-        load_words(w3, "w3", w3_words, 6, 8)
-        load_words(w2, "w2", w2_words, 2, 4)
-        load_words(w2, "w2", w2_words, 4, 6)
-        load_words(w2, "w2", w2_words, 6, 8)
+        load_words(w1, "w1", w1_words, PAIRS[2])
+        load_words(w3, "w3", w3_words, PAIRS[1])
+        load_words(w1, "w1", w1_words, PAIRS[3])
+        load_words(w3, "w3", w3_words, PAIRS[2])
+        load_words(w2, "w2", w2_words, PAIRS[0])
+        load_words(w3, "w3", w3_words, PAIRS[3])
+        for pair in PAIRS[1:]:
+            load_words(w2, "w2", w2_words, pair)
 
-        for raw, (lo, mid, hi) in zip(x_raw, X_CHUNKS):
+        for raw, (first, split, end) in zip(x_raw, X_LOADS):
             nc.scalar.copy(
-                out=x_grouped[:, mid:hi, :],
-                in_=raw[:, :, mid - lo :].rearrange("p j w -> p w j"),
+                out=x_grouped[:, split:end, :],
+                in_=raw[:, :, split - first :].rearrange("p j w -> p w j"),
             )
             nc.vector.tensor_copy(
-                out=x_grouped[:, lo:mid, :],
-                in_=raw[:, :, : mid - lo].rearrange("p j w -> p w j"),
+                out=x_grouped[:, first:split, :],
+                in_=raw[:, :, : split - first].rearrange("p j w -> p w j"),
             )
+        for first, end in X_QUANTISED:
             nc.vector.quantize_mx(
-                out=x_codes[:, lo:hi].bitcast(FP8X4),
-                scales=x_scales[:, lo:hi],
-                in_=x_grouped[:, lo:hi, :].rearrange("p w j -> p (w j)"),
+                out=x_codes[:, first:end].bitcast(FP8X4),
+                scales=x_scales[:, first:end],
+                in_=x_grouped[:, first:end, :].rearrange("p w j -> p (w j)"),
             )
 
-        def gather(first, last):
-            cols = slice(first % HELD * C, (first % HELD + last - first) * C)
-            entries = offsets[:, first * C // 16 : last * C // 16]
-            nc.vector.tensor_copy(out=s_codes[:, cols], in_=x_codes[:].indirect(entries))
-            nc.vector.tensor_copy(out=s_scales[:, cols], in_=x_scales[:].indirect(entries))
+        sig, b_bank, h, hT, h_codes, h_scales, y_parts = {}, {}, {}, {}, {}, {}, {}
 
-        sig, h, hT, codes, scales, staged = {}, {}, {}, {}, {}, {}
+        def held_columns(experts):
+            return slice(experts[0] % HELD * C, (experts[-1] % HELD + 1) * C)
 
-        def project(e, bank, w, sc):
-            cols = slice(e % HELD * C, (e % HELD + 1) * C)
+        def place_in_group(e):
+            return [(group, group.index(e)) for group in GROUPS if e in group][0]
+
+        def gather(pair):
+            entries = offsets[:, pair[0] * C // 16 : (pair[-1] + 1) * C // 16]
+            nc.vector.tensor_copy(out=slot_codes[:, held_columns(pair)], in_=x_codes[:].indirect(entries))
+            nc.vector.tensor_copy(out=slot_scales[:, held_columns(pair)], in_=x_scales[:].indirect(entries))
+
+        def first_product(e, words, scale_tile):
+            bank = free_banks.pop(0)
             nc.tensor.matmul_mx(
                 out=bank[:],
-                lhsT=s_codes[:, cols].bitcast(FP8X4),
-                lhsT_scale=s_scales[:, cols],
-                rhs=w[e].bitcast(FP4X4),
-                rhs_scale=sc[:, e, :],
+                lhsT=slot_codes[:, held_columns([e])].bitcast(FP8X4),
+                lhsT_scale=slot_scales[:, held_columns([e])],
+                rhs=words[e].bitcast(FP4X4),
+                rhs_scale=scale_tile[:, e, :],
                 start=True,
                 stop=True,
             )
+            return bank
 
-        def a_step(e):
-            bank = banks[(6, 7, 0, 1, 6, 7, 0, 1)[e]]
-            project(e, bank, w1, w1_sc)
-            sig[e] = keep.tile([P, 2, P, 2], F32, name=f"sig{e}")
-            nc.scalar.activation(sig[e][:], bank[:].rearrange("p (q u d) -> p u q d", u=2, d=2), SIGMOID)
+        def sigmoid_branch(experts):
+            for e in experts:
+                bank = first_product(e, w1, w1_sc)
+                sig[e] = keep.tile([P, 2, P, 2], F32, name=f"sig{e}")
+                nc.scalar.activation(sig[e][:], bank[:].rearrange("p (q u d) -> p u q d", u=2, d=2), SIGMOID)
+                free_banks.append(bank)
 
-        def b_step(e):
-            project(e, banks[B_BANKS[e]], w3, w3_sc)
+        def linear_branch(experts):
+            for e in experts:
+                b_bank[e] = first_product(e, w3, w3_sc)
 
-        def gate(e, pieces=1):
-            g, i = [(g, group.index(e)) for g, group in enumerate(GROUPS) if e in group][0]
-            if i == 0:
-                h[g] = keep.tile([P, len(GROUPS[g]), 2, P, 2], BF16, name=f"h{g}")
-            b = banks[B_BANKS[e]][:].rearrange("p (q u d) -> p u q d", u=2, d=2)
-            for u in range(0, 2, 2 // pieces):
-                part = slice(u, u + 2 // pieces)
-                nc.vector.tensor_tensor(h[g][:, i, part], b[:, part], sig[e][:, part], MULT)
+        def gate(group):
+            h[group] = keep.tile([P, len(group), 2, P, 2], BF16, name=f"h{group[0]}")
+            for i, e in enumerate(group):
+                b = b_bank[e][:].rearrange("p (q u d) -> p u q d", u=2, d=2)
+                for part in (slice(0, 1), slice(1, 2)) if e == E - 1 else (slice(0, 2),):
+                    nc.vector.tensor_tensor(h[group][:, i, part], b[:, part], sig[e][:, part], MULT)
+                free_banks.append(b_bank[e])
 
-        def turn(g, engine):
-            n = len(GROUPS[g])
-            bank = banks[(4, 5, 1, 4, 2)[g]][:, : n * 2 * P].rearrange("p (g u c) -> p g u c", g=n, u=2)
-            words = h[g][:].rearrange("p g u q d -> p (g u q d)").bitcast(F32)
+        def turn(group, copy):
+            n = len(group)
+            bank = free_banks.pop(0)
+            turned = bank[:, : n * 2 * P].rearrange("p (g u c) -> p g u c", g=n, u=2)
+            words = h[group][:].rearrange("p g u q d -> p (g u q d)").bitcast(F32)
             for j in range(2 * n):
-                nc.tensor.transpose(bank[:, j // 2, j % 2, :], words[:, j * P : (j + 1) * P], ident[:])
-            hT[g] = keep.tile([P, n * C * PACK], BF16, name=f"hT{g}", align_bytes=64)
-            dst = hT[g][:].bitcast(F32).rearrange("p (g c u) -> p g c u", g=n, u=2)
-            engine(out=dst, in_=bank.rearrange("p g u c -> p g c u"))
+                nc.tensor.transpose(turned[:, j // 2, j % 2, :], words[:, j * P : (j + 1) * P], ident[:])
+            hT[group] = keep.tile([P, n * C * PACK], BF16, name=f"hT{group[0]}", align_bytes=64)
+            copy(
+                out=hT[group][:].bitcast(F32).rearrange("p (g c u) -> p g c u", g=n, u=2),
+                in_=turned.rearrange("p g u c -> p g c u"),
+            )
+            free_banks.append(bank)
 
-        def y_places(e):
-            if e == E - 1:
-                return [(banks[0], 0, 2), (banks[5], 2, 1)]
-            return [(banks[(6, 7, 5, 6, 7, 1, 3)[e]], 0, 3)]
+        def quantise(group):
+            n = len(group)
+            h_codes[group] = keep.tile([P, n * C], U32, name=f"h_codes{group[0]}", align_bytes=64)
+            h_scales[group] = keep.tile([P, n * C], U8, name=f"h_scales{group[0]}", align_bytes=64)
+            nc.vector.quantize_mx(out=h_codes[group][:].bitcast(FP8X4), scales=h_scales[group][:], in_=hT[group][:])
 
-        def quantise(g):
-            n = len(GROUPS[g])
-            codes[g] = keep.tile([P, n * C], U32, name=f"h_codes{g}", align_bytes=64)
-            scales[g] = keep.tile([P, n * C], U8, name=f"h_scales{g}", align_bytes=64)
-            nc.vector.quantize_mx(out=codes[g][:].bitcast(FP8X4), scales=scales[g][:], in_=hT[g][:])
+        def second_product(experts):
+            for e in experts:
+                group, i = place_in_group(e)
+                parts = [(0, N_TILES - 1), (N_TILES - 1, 1)] if e == E - 1 else [(0, N_TILES)]
+                y_parts[e] = [(free_banks.pop(0), first, count) for first, count in parts]
+                for bank, first, count in y_parts[e]:
+                    for j in range(count):
+                        m = first + j
+                        nc.tensor.matmul_mx(
+                            out=bank[:, j * C : (j + 1) * C],
+                            lhsT=w2[e][:, 2 * P * m : 2 * P * (m + 1)].bitcast(FP4X4),
+                            lhsT_scale=w2_sc[:, e, P * m : P * (m + 1)],
+                            rhs=h_codes[group][:, i * C : (i + 1) * C].bitcast(FP8X4),
+                            rhs_scale=h_scales[group][:, i * C : (i + 1) * C],
+                            start=True,
+                            stop=True,
+                        )
 
-        def y_step(e):
-            g, i = [(g, group.index(e)) for g, group in enumerate(GROUPS) if e in group][0]
-            for bank, first, count in y_places(e):
-                for j in range(count):
-                    m = first + j
-                    nc.tensor.matmul_mx(
-                        out=bank[:, j * C : (j + 1) * C],
-                        lhsT=w2[e][:, 2 * P * m : 2 * P * (m + 1)].bitcast(FP4X4),
-                        lhsT_scale=w2_sc[:, e, P * m : P * (m + 1)],
-                        rhs=codes[g][:, i * C : (i + 1) * C].bitcast(FP8X4),
-                        rhs_scale=scales[g][:, i * C : (i + 1) * C],
-                        start=True,
-                        stop=True,
-                    )
-
-        def finish(e, *engines):
-            store = [s for s in STORES if e in s][0]
-            n = len(store)
-            if e == store[0]:
-                staged[store] = keep.tile([P, N_TILES, R, n, WIDTH], F32, name=f"staged{e}")
-            for engine, (bank, first, count) in zip(engines, y_places(e)):
-                engine(
-                    out=staged[store][:, first : first + count, :, e - store[0], :],
+        def store(pair, copies):
+            staged = keep.tile([P, N_TILES, R, len(pair), WIDTH], F32, name=f"staged{pair[0]}")
+            parts = [(i, part) for i, e in enumerate(pair) for part in y_parts[e]]
+            for copy, (i, (bank, first, count)) in zip(copies, parts):
+                copy(
+                    out=staged[:, first : first + count, :, i, :],
                     in_=bank[:, : count * C].rearrange("p (m r u) -> p m r u", r=R, u=WIDTH),
                 )
-            if e == store[-1]:
-                for r in range(R):
-                    lo = r * (SLOTS // R) + store[0] * WIDTH
-                    nc.sync.dma_start(
-                        out=out[:, lo : lo + n * WIDTH].rearrange("(m p) w -> p m w", p=P),
-                        in_=staged[store][:, :, r, :, :].rearrange("p m g u -> p m (g u)"),
-                    )
+                free_banks.append(bank)
+            for r in range(R):
+                column = r * (SLOTS // R) + pair[0] * WIDTH
+                nc.sync.dma_start(
+                    out=out[:, column : column + len(pair) * WIDTH].rearrange("(m p) w -> p m w", p=P),
+                    in_=staged[:, :, r, :, :].rearrange("p m g u -> p m (g u)"),
+                )
 
         scalar, vector = nc.scalar.copy, nc.vector.tensor_copy
-        gather(0, 1)
-        gather(1, 2)
-        gather(2, 4)
-        gather(4, 6)
-        a_step(0)
-        a_step(1)
-        b_step(0)
-        b_step(1)
-        a_step(2)
-        a_step(3)
-        gate(0)
-        gate(1)
-        turn(0, scalar)
-        gather(6, 8)
-        a_step(4)
-        a_step(5)
-        b_step(2)
-        b_step(3)
-        a_step(6)
-        a_step(7)
-        b_step(4)
-        quantise(0)
-        gate(2)
-        b_step(5)
-        gate(3)
-        turn(1, scalar)
-        y_step(0)
-        y_step(1)
-        b_step(6)
-        b_step(7)
-        finish(0, scalar)
-        finish(1, scalar)
-        quantise(1)
-        y_step(2)
-        y_step(3)
-        gate(4)
-        gate(5)
-        turn(2, scalar)
-        finish(2, scalar)
-        finish(3, scalar)
-        gate(6)
-        turn(3, vector)
-        quantise(2)
-        y_step(4)
-        y_step(5)
-        gate(7, 2)
-        turn(4, vector)
-        quantise(3)
-        y_step(6)
-        quantise(4)
-        y_step(7)
-        finish(4, scalar)
-        finish(5, vector)
-        finish(6, scalar)
-        finish(7, scalar, vector)
+
+        for pair in PAIRS[:-1]:
+            gather(pair)
+        sigmoid_branch(PAIRS[0])
+        linear_branch(PAIRS[0])
+        sigmoid_branch(PAIRS[1])
+        gate(GROUPS[0])
+        turn(GROUPS[0], scalar)
+        gather(PAIRS[-1])
+
+        sigmoid_branch(PAIRS[2])
+        linear_branch(PAIRS[1])
+        sigmoid_branch(PAIRS[3])
+        linear_branch(PAIRS[2])
+
+        quantise(GROUPS[0])
+        gate(GROUPS[1])
+        turn(GROUPS[1], scalar)
+        second_product(PAIRS[0])
+        linear_branch(PAIRS[3])
+        quantise(GROUPS[1])
+        second_product(PAIRS[1])
+        gate(GROUPS[2])
+        store(PAIRS[0], (scalar, scalar))
+        turn(GROUPS[2], scalar)
+        store(PAIRS[1], (scalar, scalar))
+
+        gate(GROUPS[3])
+        turn(GROUPS[3], vector)
+        quantise(GROUPS[2])
+        second_product(PAIRS[2])
+        gate(GROUPS[4])
+        turn(GROUPS[4], vector)
+        for group in GROUPS[3:]:
+            quantise(group)
+            second_product(group)
+        store(PAIRS[2], (scalar, vector))
+        store(PAIRS[3], (scalar, vector, scalar))

@@ -24,8 +24,8 @@ FP4X4 = mybir.dt.float4_e2m1fn_x4
 MULT = mybir.AluOpType.mult
 SIGMOID = mybir.ActivationFunctionType.Sigmoid
 
-X_LOADS = [(0, 256, 384), (384, 472, 512)]
-X_QUANTISED = [(0, 256), (256, 384), (384, 512)]
+X_LOADS = [(0, 344, 512)]
+X_QUANTISED = [(0, 256), (256, 512)]
 PAIRS = [(0, 1), (2, 3), (4, 5), (6, 7)]
 GROUPS = [(0, 1), (2, 3), (4, 5), (6,), (7,)]
 HELD = 6
@@ -95,10 +95,11 @@ def tile_moe_eps_glu_sigmoid_kernel(
                 out=x_grouped[:, split:end, :],
                 in_=raw[:, :, split - first :].rearrange("p j w -> p w j"),
             )
-            nc.vector.tensor_copy(
-                out=x_grouped[:, first:split, :],
-                in_=raw[:, :, : split - first].rearrange("p j w -> p w j"),
-            )
+            for a, b in ((first, T // 2), (T // 2, split)):
+                nc.vector.tensor_copy(
+                    out=x_grouped[:, a:b, :],
+                    in_=raw[:, :, a - first : b - first].rearrange("p j w -> p w j"),
+                )
         for first, end in X_QUANTISED:
             nc.vector.quantize_mx(
                 out=x_codes[:, first:end].bitcast(FP8X4),
@@ -242,5 +243,4 @@ def tile_moe_eps_glu_sigmoid_kernel(
         for group in GROUPS[3:]:
             quantise(group)
             second_product(group)
-        store(PAIRS[2], (scalar, vector))
-        store(PAIRS[3], (scalar, vector, scalar))
+        store(PAIRS[2] + PAIRS[3], (scalar, vector, scalar, vector, scalar))

@@ -28,7 +28,7 @@ X_LOADS = [(0, 344, 512)]
 X_QUANTISED = [(0, 256), (256, 512)]
 PAIRS = [(0, 1), (2, 3), (4, 5), (6, 7)]
 GROUPS = [(0, 1), (2, 3), (4, 5), (6,), (7,)]
-HELD = 6
+HELD = 8
 
 
 def tile_moe_eps_glu_sigmoid_kernel(
@@ -48,7 +48,7 @@ def tile_moe_eps_glu_sigmoid_kernel(
         slot_scales = keep.tile([P, HELD * C], U8, name="slot_scales", align_bytes=64)
         w1_sc = keep.tile([P, E, H], U8, name="w1_sc", align_bytes=64)
         w3_sc = keep.tile([P, E, H], U8, name="w3_sc", align_bytes=64)
-        w2_sc = keep.tile([P, E, N], U8, name="w2_sc", align_bytes=64)
+        w2_sc = [keep.tile([P, E // 2, N], U8, name=f"w2_sc{i}", align_bytes=64) for i in range(2)]
         ident = keep.tile([P, P], F32, name="ident")
         free_banks = [psum.tile([P, H], F32, name=f"bank{b}") for b in range(BANKS)]
 
@@ -56,7 +56,7 @@ def tile_moe_eps_glu_sigmoid_kernel(
             nc.sync.dma_start(out=raw[:], in_=xT[:, first:end].rearrange("(p j) w -> p j w", j=PACK))
         nc.sync.dma_start(offsets[:], offs)
 
-        for scale_tile in (w1_sc, x_scales, w3_sc, w2_sc):
+        for scale_tile in (w1_sc, x_scales, w3_sc, *w2_sc):
             nc.vector.memset(scale_tile[:].bitcast(I32), 0)
         make_identity(nc, ident[:])
 
@@ -77,18 +77,20 @@ def tile_moe_eps_glu_sigmoid_kernel(
 
         load_scales(w1_sc, w1_scales)
         load_words(w1, "w1", w1_words, PAIRS[0])
-        load_scales(w3_sc, w3_scales)
-        load_words(w3, "w3", w3_words, PAIRS[0])
         load_words(w1, "w1", w1_words, PAIRS[1])
-        load_scales(w2_sc, w2_scales)
+        load_scales(w3_sc, w3_scales)
+        load_scales(w2_sc[0], w2_scales[: E // 2])
+        load_words(w3, "w3", w3_words, PAIRS[0])
         load_words(w1, "w1", w1_words, PAIRS[2])
         load_words(w3, "w3", w3_words, PAIRS[1])
         load_words(w1, "w1", w1_words, PAIRS[3])
         load_words(w3, "w3", w3_words, PAIRS[2])
         load_words(w2, "w2", w2_words, PAIRS[0])
         load_words(w3, "w3", w3_words, PAIRS[3])
-        for pair in PAIRS[1:]:
-            load_words(w2, "w2", w2_words, pair)
+        load_words(w2, "w2", w2_words, PAIRS[1])
+        load_scales(w2_sc[1], w2_scales[E // 2 :])
+        load_words(w2, "w2", w2_words, PAIRS[2])
+        load_words(w2, "w2", w2_words, PAIRS[3])
 
         for raw, (first, split, end) in zip(x_raw, X_LOADS):
             nc.scalar.copy(
@@ -183,7 +185,7 @@ def tile_moe_eps_glu_sigmoid_kernel(
                         nc.tensor.matmul_mx(
                             out=bank[:, j * C : (j + 1) * C],
                             lhsT=w2[e][:, 2 * P * m : 2 * P * (m + 1)].bitcast(FP4X4),
-                            lhsT_scale=w2_sc[:, e, P * m : P * (m + 1)],
+                            lhsT_scale=w2_sc[e // (E // 2)][:, e % (E // 2), P * m : P * (m + 1)],
                             rhs=h_codes[group][:, i * C : (i + 1) * C].bitcast(FP8X4),
                             rhs_scale=h_scales[group][:, i * C : (i + 1) * C],
                             start=True,
@@ -208,39 +210,35 @@ def tile_moe_eps_glu_sigmoid_kernel(
 
         scalar, vector = nc.scalar.copy, nc.vector.tensor_copy
 
-        for pair in PAIRS[:-1]:
+        for pair in PAIRS:
             gather(pair)
         sigmoid_branch(PAIRS[0])
-        linear_branch(PAIRS[0])
         sigmoid_branch(PAIRS[1])
-        gate(GROUPS[0])
-        turn(GROUPS[0], scalar)
-        gather(PAIRS[-1])
-
+        linear_branch(PAIRS[0])
         sigmoid_branch(PAIRS[2])
         linear_branch(PAIRS[1])
-        sigmoid_branch(PAIRS[3])
-        linear_branch(PAIRS[2])
-
-        quantise(GROUPS[0])
+        gate(GROUPS[0])
+        turn(GROUPS[0], scalar)
         gate(GROUPS[1])
+        sigmoid_branch(PAIRS[3])
+        quantise(GROUPS[0])
+        linear_branch(PAIRS[2])
         turn(GROUPS[1], scalar)
         second_product(PAIRS[0])
+        gate(GROUPS[2])
         linear_branch(PAIRS[3])
         quantise(GROUPS[1])
-        second_product(PAIRS[1])
-        gate(GROUPS[2])
         store(PAIRS[0], (scalar, scalar))
         turn(GROUPS[2], scalar)
-        store(PAIRS[1], (scalar, scalar))
-
+        second_product(PAIRS[1])
         gate(GROUPS[3])
-        turn(GROUPS[3], vector)
-        quantise(GROUPS[2])
-        second_product(PAIRS[2])
         gate(GROUPS[4])
+        quantise(GROUPS[2])
+        turn(GROUPS[3], vector)
         turn(GROUPS[4], vector)
+        store(PAIRS[1], (scalar, scalar))
+        second_product(PAIRS[2])
         for group in GROUPS[3:]:
             quantise(group)
             second_product(group)
-        store(PAIRS[2] + PAIRS[3], (scalar, vector, scalar, vector, scalar))
+        store(PAIRS[2] + PAIRS[3], (scalar, scalar, vector, scalar, vector))

@@ -208,6 +208,37 @@ def tile_moe_eps_glu_sigmoid_kernel(
                     in_=staged[:, :, r, :, :].rearrange("p m g u -> p m (g u)"),
                 )
 
+        def result_block(bank, column, e, m):
+            group, i = place_in_group(e)
+            nc.tensor.matmul_mx(
+                out=bank[:, column : column + C],
+                lhsT=w2[e][:, 2 * P * m : 2 * P * (m + 1)].bitcast(FP4X4),
+                lhsT_scale=w2_sc[e // (E // 2)][:, e % (E // 2), P * m : P * (m + 1)],
+                rhs=h_codes[group][:, i * C : (i + 1) * C].bitcast(FP8X4),
+                rhs_scale=h_scales[group][:, i * C : (i + 1) * C],
+                start=True,
+                stop=True,
+            )
+
+        last = [keep.tile([P, R, E // 2, WIDTH], F32, name=f"last{m}") for m in range(N_TILES)]
+
+        def last_results(experts, copies):
+            first = experts[0] - E // 2
+            for m, copy in enumerate(copies):
+                bank = free_banks.pop(0)
+                for i, e in enumerate(experts):
+                    result_block(bank, i * C, e, m)
+                copy(
+                    out=last[m][:, :, first : first + len(experts), :],
+                    in_=bank[:, : len(experts) * C].rearrange("p (g r u) -> p r g u", r=R, u=WIDTH),
+                )
+                free_banks.append(bank)
+
+        def store_last():
+            for m in range(N_TILES):
+                rows = out[m * P : (m + 1) * P, :].rearrange("p (r w) -> p r w", r=R)
+                nc.sync.dma_start(out=rows[:, :, E // 2 * WIDTH :], in_=last[m][:].rearrange("p r g u -> p r (g u)"))
+
         scalar, vector = nc.scalar.copy, nc.vector.tensor_copy
 
         for pair in PAIRS:
@@ -237,8 +268,8 @@ def tile_moe_eps_glu_sigmoid_kernel(
         turn(GROUPS[3], vector)
         turn(GROUPS[4], vector)
         store(PAIRS[1], (scalar, scalar))
-        second_product(PAIRS[2])
-        for group in GROUPS[3:]:
-            quantise(group)
-            second_product(group)
-        store(PAIRS[2] + PAIRS[3], (scalar, scalar, vector, scalar, vector))
+        last_results(PAIRS[2], (scalar, scalar, scalar))
+        quantise(GROUPS[3])
+        quantise(GROUPS[4])
+        last_results(PAIRS[3], (vector, scalar, vector))
+        store_last()

@@ -28,7 +28,8 @@ X_LOADS = [(0, 344, 512)]
 X_QUANTISED = [(0, 256), (256, 512)]
 PAIRS = [(0, 1), (2, 3), (4, 5), (6, 7)]
 GROUPS = [(0, 1), (2, 3), (4, 5), (6,), (7,)]
-HELD = 8
+HELD = 7
+GATHERS = [(0, 1), (2, 3), (4, 5, 6), (7,)]
 
 
 def tile_moe_eps_glu_sigmoid_kernel(
@@ -109,7 +110,7 @@ def tile_moe_eps_glu_sigmoid_kernel(
                 in_=x_grouped[:, first:end, :].rearrange("p w j -> p (w j)"),
             )
 
-        sig, b_bank, h, hT, h_codes, h_scales, y_parts = {}, {}, {}, {}, {}, {}, {}
+        sig, b_bank, h, hT, h_codes, h_scales = {}, {}, {}, {}, {}, {}
 
         def held_columns(experts):
             return slice(experts[0] % HELD * C, (experts[-1] % HELD + 1) * C)
@@ -174,40 +175,6 @@ def tile_moe_eps_glu_sigmoid_kernel(
             h_scales[group] = keep.tile([P, n * C], U8, name=f"h_scales{group[0]}", align_bytes=64)
             nc.vector.quantize_mx(out=h_codes[group][:].bitcast(FP8X4), scales=h_scales[group][:], in_=hT[group][:])
 
-        def second_product(experts):
-            for e in experts:
-                group, i = place_in_group(e)
-                parts = [(0, N_TILES - 1), (N_TILES - 1, 1)] if e == E - 1 else [(0, N_TILES)]
-                y_parts[e] = [(free_banks.pop(0), first, count) for first, count in parts]
-                for bank, first, count in y_parts[e]:
-                    for j in range(count):
-                        m = first + j
-                        nc.tensor.matmul_mx(
-                            out=bank[:, j * C : (j + 1) * C],
-                            lhsT=w2[e][:, 2 * P * m : 2 * P * (m + 1)].bitcast(FP4X4),
-                            lhsT_scale=w2_sc[e // (E // 2)][:, e % (E // 2), P * m : P * (m + 1)],
-                            rhs=h_codes[group][:, i * C : (i + 1) * C].bitcast(FP8X4),
-                            rhs_scale=h_scales[group][:, i * C : (i + 1) * C],
-                            start=True,
-                            stop=True,
-                        )
-
-        def store(pair, copies):
-            staged = keep.tile([P, N_TILES, R, len(pair), WIDTH], F32, name=f"staged{pair[0]}")
-            parts = [(i, part) for i, e in enumerate(pair) for part in y_parts[e]]
-            for copy, (i, (bank, first, count)) in zip(copies, parts):
-                copy(
-                    out=staged[:, first : first + count, :, i, :],
-                    in_=bank[:, : count * C].rearrange("p (m r u) -> p m r u", r=R, u=WIDTH),
-                )
-                free_banks.append(bank)
-            for r in range(R):
-                column = r * (SLOTS // R) + pair[0] * WIDTH
-                nc.sync.dma_start(
-                    out=out[:, column : column + len(pair) * WIDTH].rearrange("(m p) w -> p m w", p=P),
-                    in_=staged[:, :, r, :, :].rearrange("p m g u -> p m (g u)"),
-                )
-
         def result_block(bank, column, e, m):
             group, i = place_in_group(e)
             nc.tensor.matmul_mx(
@@ -220,56 +187,85 @@ def tile_moe_eps_glu_sigmoid_kernel(
                 stop=True,
             )
 
-        last = [keep.tile([P, R, E // 2, WIDTH], F32, name=f"last{m}") for m in range(N_TILES)]
+        def second_product(pair):
+            banks = [free_banks.pop(0) for e in pair]
+            for bank, e in zip(banks, pair):
+                for m in range(N_TILES):
+                    result_block(bank, m * C, e, m)
+            return banks
 
-        def last_results(experts, copies):
-            first = experts[0] - E // 2
-            for m, copy in enumerate(copies):
-                bank = free_banks.pop(0)
-                for i, e in enumerate(experts):
-                    result_block(bank, i * C, e, m)
-                copy(
-                    out=last[m][:, :, first : first + len(experts), :],
-                    in_=bank[:, : len(experts) * C].rearrange("p (g r u) -> p r g u", r=R, u=WIDTH),
+        def store(pair, banks):
+            staged = keep.tile([P, N_TILES, R, len(pair), WIDTH], F32, name=f"staged{pair[0]}")
+            for i, bank in enumerate(banks):
+                nc.scalar.copy(
+                    out=staged[:, :, :, i, :],
+                    in_=bank[:, : N_TILES * C].rearrange("p (m r u) -> p m r u", r=R, u=WIDTH),
                 )
                 free_banks.append(bank)
+            for r in range(R):
+                column = r * (SLOTS // R) + pair[0] * WIDTH
+                nc.sync.dma_start(
+                    out=out[:, column : column + len(pair) * WIDTH].rearrange("(m p) w -> p m w", p=P),
+                    in_=staged[:, :, r, :, :].rearrange("p m g u -> p m (g u)"),
+                )
 
-        def store_last():
+        def last_results():
+            experts = PAIRS[2] + PAIRS[3]
+            n = len(experts)
+            banks = [free_banks.pop(0) for m in range(N_TILES)]
+            alone = free_banks.pop(0)
+            for i, e in enumerate(experts):
+                for m in range(N_TILES):
+                    if e == E - 1 and m == 0:
+                        result_block(alone, 0, e, m)
+                    else:
+                        result_block(banks[m], i * C, e, m)
+            staged = [keep.tile([P, R, n, WIDTH], F32, name=f"last{m}") for m in range(N_TILES)]
+            parts = [
+                (scalar, 0, banks[0], 0, n - 1),
+                (vector, 0, alone, n - 1, 1),
+                (scalar, 1, banks[1], 0, n),
+                (vector, 2, banks[2], 0, n),
+            ]
+            for copy, m, bank, first, count in parts:
+                copy(
+                    out=staged[m][:, :, first : first + count, :],
+                    in_=bank[:, : count * C].rearrange("p (g r u) -> p r g u", r=R, u=WIDTH),
+                )
             for m in range(N_TILES):
                 rows = out[m * P : (m + 1) * P, :].rearrange("p (r w) -> p r w", r=R)
-                nc.sync.dma_start(out=rows[:, :, E // 2 * WIDTH :], in_=last[m][:].rearrange("p r g u -> p r (g u)"))
+                nc.sync.dma_start(out=rows[:, :, experts[0] * WIDTH :], in_=staged[m][:].rearrange("p r g u -> p r (g u)"))
 
         scalar, vector = nc.scalar.copy, nc.vector.tensor_copy
 
-        for pair in PAIRS:
-            gather(pair)
+        for experts in GATHERS[:-1]:
+            gather(experts)
         sigmoid_branch(PAIRS[0])
         sigmoid_branch(PAIRS[1])
         linear_branch(PAIRS[0])
         sigmoid_branch(PAIRS[2])
         linear_branch(PAIRS[1])
         gate(GROUPS[0])
+        gather(GATHERS[-1])
         turn(GROUPS[0], scalar)
         gate(GROUPS[1])
         sigmoid_branch(PAIRS[3])
         quantise(GROUPS[0])
         linear_branch(PAIRS[2])
         turn(GROUPS[1], scalar)
-        second_product(PAIRS[0])
+        first = second_product(PAIRS[0])
         gate(GROUPS[2])
         linear_branch(PAIRS[3])
         quantise(GROUPS[1])
-        store(PAIRS[0], (scalar, scalar))
+        store(PAIRS[0], first)
         turn(GROUPS[2], scalar)
-        second_product(PAIRS[1])
+        second = second_product(PAIRS[1])
         gate(GROUPS[3])
         gate(GROUPS[4])
         quantise(GROUPS[2])
-        turn(GROUPS[3], vector)
+        store(PAIRS[1], second)
+        turn(GROUPS[3], scalar)
         turn(GROUPS[4], vector)
-        store(PAIRS[1], (scalar, scalar))
-        last_results(PAIRS[2], (scalar, scalar, scalar))
         quantise(GROUPS[3])
         quantise(GROUPS[4])
-        last_results(PAIRS[3], (vector, scalar, vector))
-        store_last()
+        last_results()

@@ -86,8 +86,8 @@ def tile_moe_eps_glu_sigmoid_kernel(
         load_words(w3, "w3", w3_words, PAIRS[1])
         load_words(w1, "w1", w1_words, PAIRS[3])
         load_words(w3, "w3", w3_words, PAIRS[2])
-        load_words(w2, "w2", w2_words, PAIRS[0])
         load_words(w3, "w3", w3_words, PAIRS[3])
+        load_words(w2, "w2", w2_words, PAIRS[0])
         load_words(w2, "w2", w2_words, PAIRS[1])
         load_scales(w2_sc[1], w2_scales[E // 2 :])
         load_words(w2, "w2", w2_words, PAIRS[2])

@@ -77,8 +77,7 @@ def tile_moe_eps_glu_sigmoid_kernel(
                 nc.sync.dma_start(out=tile[:].bitcast(I32)[r:P:32], in_=rows[r])
 
         load_scales(w1_sc, w1_scales)
-        load_words(w1, "w1", w1_words, PAIRS[0])
-        load_words(w1, "w1", w1_words, PAIRS[1])
+        load_words(w1, "w1", w1_words, PAIRS[0] + PAIRS[1])
         load_scales(w3_sc, w3_scales)
         load_scales(w2_sc[0], w2_scales[: E // 2])
         load_words(w3, "w3", w3_words, PAIRS[0])
@@ -90,8 +89,7 @@ def tile_moe_eps_glu_sigmoid_kernel(
         load_words(w2, "w2", w2_words, PAIRS[0])
         load_words(w2, "w2", w2_words, PAIRS[1])
         load_scales(w2_sc[1], w2_scales[E // 2 :])
-        load_words(w2, "w2", w2_words, PAIRS[2])
-        load_words(w2, "w2", w2_words, PAIRS[3])
+        load_words(w2, "w2", w2_words, PAIRS[2] + PAIRS[3])
 
         for raw, (first, split, end) in zip(x_raw, X_LOADS):
             nc.scalar.copy(
@@ -214,8 +212,10 @@ def tile_moe_eps_glu_sigmoid_kernel(
             n = len(experts)
             banks = [free_banks.pop(0) for m in range(N_TILES)]
             alone = free_banks.pop(0)
-            for i, e in enumerate(experts):
-                for m in range(N_TILES):
+            early = [(i, m) for m in range(N_TILES - 1) for i in range(n // 2)]
+            every = [(i, m) for m in range(N_TILES) for i in range(n)]
+            for i, m in early + [step for step in every if step not in early]:
+                for e in [experts[i]]:
                     if e == E - 1 and m == 0:
                         result_block(alone, 0, e, m)
                     else:

@@ -24,12 +24,12 @@ FP4X4 = mybir.dt.float4_e2m1fn_x4
 MULT = mybir.AluOpType.mult
 SIGMOID = mybir.ActivationFunctionType.Sigmoid
 
-X_LOADS = [(0, 344, 512)]
-X_QUANTISED = [(0, 256), (256, 512)]
+X_LOADS = [(0, 256, 384), (384, 472, 512)]
+X_QUANTISED = [(0, 256), (256, 384), (384, 512)]
 PAIRS = [(0, 1), (2, 3), (4, 5), (6, 7)]
 GROUPS = [(0, 1), (2, 3), (4, 5), (6,), (7,)]
-HELD = 7
-GATHERS = [(0, 1), (2, 3), (4, 5, 6), (7,)]
+GATHERS = PAIRS
+HELD = E
 
 
 def tile_moe_eps_glu_sigmoid_kernel(
@@ -41,7 +41,7 @@ def tile_moe_eps_glu_sigmoid_kernel(
         psum = ctx.enter_context(tc.psum_pool(name="psum", bufs=1))
 
         offsets = keep.tile([P, SLOTS // 16], U16, name="offsets")
-        x_raw = [keep.tile([P, PACK, end - first], F32, name=f"x_raw{first}") for first, split, end in X_LOADS]
+        x_raw = [keep.tile([P, PACK, end - start], F32, name=f"x_raw{start}") for start, split, end in X_LOADS]
         x_grouped = keep.tile([P, T, PACK], BF16, name="x_grouped", align_bytes=64)
         x_codes = keep.tile([P, T], U32, name="x_codes", align_bytes=64)
         x_scales = keep.tile([P, T], U8, name="x_scales", align_bytes=64)
@@ -49,12 +49,12 @@ def tile_moe_eps_glu_sigmoid_kernel(
         slot_scales = keep.tile([P, HELD * C], U8, name="slot_scales", align_bytes=64)
         w1_sc = keep.tile([P, E, H], U8, name="w1_sc", align_bytes=64)
         w3_sc = keep.tile([P, E, H], U8, name="w3_sc", align_bytes=64)
-        w2_sc = [keep.tile([P, E // 2, N], U8, name=f"w2_sc{i}", align_bytes=64) for i in range(2)]
+        w2_sc = [keep.tile([P, E // 2, N], U8, name=f"w2_sc{half}", align_bytes=64) for half in range(2)]
         ident = keep.tile([P, P], F32, name="ident")
-        free_banks = [psum.tile([P, H], F32, name=f"bank{b}") for b in range(BANKS)]
+        free_banks = [psum.tile([P, H], F32, name=f"bank{number}") for number in range(BANKS)]
 
-        for raw, (first, split, end) in zip(x_raw, X_LOADS):
-            nc.sync.dma_start(out=raw[:], in_=xT[:, first:end].rearrange("(p j) w -> p j w", j=PACK))
+        for raw, (start, split, end) in zip(x_raw, X_LOADS):
+            nc.sync.dma_start(out=raw[:], in_=xT[:, start:end].rearrange("(p t) w -> p t w", t=PACK))
         nc.sync.dma_start(offsets[:], offs)
 
         for scale_tile in (w1_sc, x_scales, w3_sc, *w2_sc):
@@ -63,18 +63,18 @@ def tile_moe_eps_glu_sigmoid_kernel(
 
         w1, w3, w2 = {}, {}, {}
 
-        def load_words(table, name, words, pair):
-            tile = keep.tile([P, len(pair), words.shape[3]], U8, name=f"{name}_{pair[0]}", align_bytes=64)
+        def load_words(table, name, words, experts):
+            tile = keep.tile([P, len(experts), words.shape[3]], U8, name=f"{name}_{experts[0]}", align_bytes=64)
             nc.sync.dma_start(
                 out=tile[:].bitcast(I32),
-                in_=words[pair[0] : pair[-1] + 1].bitcast(I32).rearrange("e s p w -> p (e s) w"),
+                in_=words[experts[0] : experts[-1] + 1].bitcast(I32).rearrange("e s p w -> p (e s) w"),
             )
-            table.update({e: tile[:, i, :] for i, e in enumerate(pair)})
+            table.update({e: tile[:, place, :] for place, e in enumerate(experts)})
 
         def load_scales(tile, scales):
-            rows = scales.bitcast(I32).rearrange("e s (q r) w -> r q (e s) w", r=4)
-            for r in range(4):
-                nc.sync.dma_start(out=tile[:].bitcast(I32)[r:P:32], in_=rows[r])
+            rows = scales.bitcast(I32).rearrange("e s (high low) w -> low high (e s) w", low=4)
+            for low in range(4):
+                nc.sync.dma_start(out=tile[:].bitcast(I32)[low:P:32], in_=rows[low])
 
         load_scales(w1_sc, w1_scales)
         load_words(w1, "w1", w1_words, PAIRS[0] + PAIRS[1])
@@ -91,21 +91,16 @@ def tile_moe_eps_glu_sigmoid_kernel(
         load_scales(w2_sc[1], w2_scales[E // 2 :])
         load_words(w2, "w2", w2_words, PAIRS[2] + PAIRS[3])
 
-        for raw, (first, split, end) in zip(x_raw, X_LOADS):
-            nc.scalar.copy(
-                out=x_grouped[:, split:end, :],
-                in_=raw[:, :, split - first :].rearrange("p j w -> p w j"),
+        for raw, (start, split, end) in zip(x_raw, X_LOADS):
+            nc.scalar.copy(out=x_grouped[:, split:end, :], in_=raw[:, :, split - start :].rearrange("p t w -> p w t"))
+            nc.vector.tensor_copy(
+                out=x_grouped[:, start:split, :], in_=raw[:, :, : split - start].rearrange("p t w -> p w t")
             )
-            for a, b in ((first, T // 2), (T // 2, split)):
-                nc.vector.tensor_copy(
-                    out=x_grouped[:, a:b, :],
-                    in_=raw[:, :, a - first : b - first].rearrange("p j w -> p w j"),
-                )
-        for first, end in X_QUANTISED:
+        for start, end in X_QUANTISED:
             nc.vector.quantize_mx(
-                out=x_codes[:, first:end].bitcast(FP8X4),
-                scales=x_scales[:, first:end],
-                in_=x_grouped[:, first:end, :].rearrange("p w j -> p (w j)"),
+                out=x_codes[:, start:end].bitcast(FP8X4),
+                scales=x_scales[:, start:end],
+                in_=x_grouped[:, start:end, :].rearrange("p w t -> p (w t)"),
             )
 
         sig, b_bank, h, hT, h_codes, h_scales = {}, {}, {}, {}, {}, {}
@@ -116,10 +111,10 @@ def tile_moe_eps_glu_sigmoid_kernel(
         def place_in_group(e):
             return [(group, group.index(e)) for group in GROUPS if e in group][0]
 
-        def gather(pair):
-            entries = offsets[:, pair[0] * C // 16 : (pair[-1] + 1) * C // 16]
-            nc.vector.tensor_copy(out=slot_codes[:, held_columns(pair)], in_=x_codes[:].indirect(entries))
-            nc.vector.tensor_copy(out=slot_scales[:, held_columns(pair)], in_=x_scales[:].indirect(entries))
+        def gather(experts):
+            entries = offsets[:, experts[0] * C // 16 : (experts[-1] + 1) * C // 16]
+            nc.vector.tensor_copy(out=slot_codes[:, held_columns(experts)], in_=x_codes[:].indirect(entries))
+            nc.vector.tensor_copy(out=slot_scales[:, held_columns(experts)], in_=x_scales[:].indirect(entries))
 
         def first_product(e, words, scale_tile):
             bank = free_banks.pop(0)
@@ -147,40 +142,42 @@ def tile_moe_eps_glu_sigmoid_kernel(
 
         def gate(group):
             h[group] = keep.tile([P, len(group), 2, P, 2], BF16, name=f"h{group[0]}")
-            for i, e in enumerate(group):
+            for place, e in enumerate(group):
                 b = b_bank[e][:].rearrange("p (q u d) -> p u q d", u=2, d=2)
                 for part in (slice(0, 1), slice(1, 2)) if e == E - 1 else (slice(0, 2),):
-                    nc.vector.tensor_tensor(h[group][:, i, part], b[:, part], sig[e][:, part], MULT)
+                    nc.vector.tensor_tensor(h[group][:, place, part], b[:, part], sig[e][:, part], MULT)
                 free_banks.append(b_bank[e])
 
         def turn(group, copy):
-            n = len(group)
+            size = len(group)
             bank = free_banks.pop(0)
-            turned = bank[:, : n * 2 * P].rearrange("p (g u c) -> p g u c", g=n, u=2)
-            words = h[group][:].rearrange("p g u q d -> p (g u q d)").bitcast(F32)
-            for j in range(2 * n):
-                nc.tensor.transpose(turned[:, j // 2, j % 2, :], words[:, j * P : (j + 1) * P], ident[:])
-            hT[group] = keep.tile([P, n * C * PACK], BF16, name=f"hT{group[0]}", align_bytes=64)
+            turned = bank[:, : size * 2 * P].rearrange("p (e u c) -> p e u c", e=size, u=2)
+            pairs_of_i = h[group][:].rearrange("p e u q d -> p (e u q d)").bitcast(F32)
+            for place in range(size):
+                for u in range(2):
+                    column = (2 * place + u) * P
+                    nc.tensor.transpose(turned[:, place, u, :], pairs_of_i[:, column : column + P], ident[:])
+            hT[group] = keep.tile([P, size * C * PACK], BF16, name=f"hT{group[0]}", align_bytes=64)
             copy(
-                out=hT[group][:].bitcast(F32).rearrange("p (g c u) -> p g c u", g=n, u=2),
-                in_=turned.rearrange("p g u c -> p g c u"),
+                out=hT[group][:].bitcast(F32).rearrange("p (e c u) -> p e c u", e=size, u=2),
+                in_=turned.rearrange("p e u c -> p e c u"),
             )
             free_banks.append(bank)
 
         def quantise(group):
-            n = len(group)
-            h_codes[group] = keep.tile([P, n * C], U32, name=f"h_codes{group[0]}", align_bytes=64)
-            h_scales[group] = keep.tile([P, n * C], U8, name=f"h_scales{group[0]}", align_bytes=64)
+            size = len(group)
+            h_codes[group] = keep.tile([P, size * C], U32, name=f"h_codes{group[0]}", align_bytes=64)
+            h_scales[group] = keep.tile([P, size * C], U8, name=f"h_scales{group[0]}", align_bytes=64)
             nc.vector.quantize_mx(out=h_codes[group][:].bitcast(FP8X4), scales=h_scales[group][:], in_=hT[group][:])
 
         def result_block(bank, column, e, m):
-            group, i = place_in_group(e)
+            group, place = place_in_group(e)
             nc.tensor.matmul_mx(
                 out=bank[:, column : column + C],
                 lhsT=w2[e][:, 2 * P * m : 2 * P * (m + 1)].bitcast(FP4X4),
                 lhsT_scale=w2_sc[e // (E // 2)][:, e % (E // 2), P * m : P * (m + 1)],
-                rhs=h_codes[group][:, i * C : (i + 1) * C].bitcast(FP8X4),
-                rhs_scale=h_scales[group][:, i * C : (i + 1) * C],
+                rhs=h_codes[group][:, place * C : (place + 1) * C].bitcast(FP8X4),
+                rhs_scale=h_scales[group][:, place * C : (place + 1) * C],
                 start=True,
                 stop=True,
             )
@@ -194,51 +191,51 @@ def tile_moe_eps_glu_sigmoid_kernel(
 
         def store(pair, banks):
             staged = keep.tile([P, N_TILES, R, len(pair), WIDTH], F32, name=f"staged{pair[0]}")
-            for i, bank in enumerate(banks):
+            for place, bank in enumerate(banks):
                 nc.scalar.copy(
-                    out=staged[:, :, :, i, :],
-                    in_=bank[:, : N_TILES * C].rearrange("p (m r u) -> p m r u", r=R, u=WIDTH),
+                    out=staged[:, :, :, place, :],
+                    in_=bank[:, : N_TILES * C].rearrange("p (m r c) -> p m r c", r=R, c=WIDTH),
                 )
                 free_banks.append(bank)
             for r in range(R):
                 column = r * (SLOTS // R) + pair[0] * WIDTH
                 nc.sync.dma_start(
                     out=out[:, column : column + len(pair) * WIDTH].rearrange("(m p) w -> p m w", p=P),
-                    in_=staged[:, :, r, :, :].rearrange("p m g u -> p m (g u)"),
+                    in_=staged[:, :, r, :, :].rearrange("p m e c -> p m (e c)"),
                 )
 
-        def last_results():
-            experts = PAIRS[2] + PAIRS[3]
-            n = len(experts)
+        def last_results(experts):
+            size = len(experts)
             banks = [free_banks.pop(0) for m in range(N_TILES)]
-            alone = free_banks.pop(0)
-            early = [(i, m) for m in range(N_TILES - 1) for i in range(n // 2)]
-            every = [(i, m) for m in range(N_TILES) for i in range(n)]
-            for i, m in early + [step for step in every if step not in early]:
-                for e in [experts[i]]:
-                    if e == E - 1 and m == 0:
-                        result_block(alone, 0, e, m)
-                    else:
-                        result_block(banks[m], i * C, e, m)
-            staged = [keep.tile([P, R, n, WIDTH], F32, name=f"last{m}") for m in range(N_TILES)]
-            parts = [
-                (scalar, 0, banks[0], 0, n - 1),
-                (vector, 0, alone, n - 1, 1),
-                (scalar, 1, banks[1], 0, n),
-                (vector, 2, banks[2], 0, n),
-            ]
-            for copy, m, bank, first, count in parts:
+            apart = free_banks.pop(0)
+            early = [(place, m) for m in range(N_TILES - 1) for place in range(size // 2)]
+            rest = [(place, m) for m in range(N_TILES) for place in range(size) if (place, m) not in early]
+            for place, m in early + rest:
+                if (place, m) == (size - 1, 0):
+                    result_block(apart, 0, experts[place], m)
+                else:
+                    result_block(banks[m], place * C, experts[place], m)
+            staged = [keep.tile([P, R, size, WIDTH], F32, name=f"last{m}") for m in range(N_TILES)]
+
+            def stage(copy, bank, m, start, end):
                 copy(
-                    out=staged[m][:, :, first : first + count, :],
-                    in_=bank[:, : count * C].rearrange("p (g r u) -> p r g u", r=R, u=WIDTH),
+                    out=staged[m][:, :, start:end, :],
+                    in_=bank[:, : (end - start) * C].rearrange("p (e r c) -> p r e c", r=R, c=WIDTH),
                 )
+
+            stage(scalar, banks[0], 0, 0, size - 1)
+            stage(vector, apart, 0, size - 1, size)
+            stage(scalar, banks[1], 1, 0, size)
+            stage(vector, banks[2], 2, 0, size)
             for m in range(N_TILES):
                 rows = out[m * P : (m + 1) * P, :].rearrange("p (r w) -> p r w", r=R)
-                nc.sync.dma_start(out=rows[:, :, experts[0] * WIDTH :], in_=staged[m][:].rearrange("p r g u -> p r (g u)"))
+                nc.sync.dma_start(
+                    out=rows[:, :, experts[0] * WIDTH :], in_=staged[m][:].rearrange("p r e c -> p r (e c)")
+                )
 
         scalar, vector = nc.scalar.copy, nc.vector.tensor_copy
 
-        for experts in GATHERS[:-1]:
+        for experts in GATHERS:
             gather(experts)
         sigmoid_branch(PAIRS[0])
         sigmoid_branch(PAIRS[1])
@@ -246,26 +243,25 @@ def tile_moe_eps_glu_sigmoid_kernel(
         sigmoid_branch(PAIRS[2])
         linear_branch(PAIRS[1])
         gate(GROUPS[0])
-        gather(GATHERS[-1])
         turn(GROUPS[0], scalar)
         gate(GROUPS[1])
         sigmoid_branch(PAIRS[3])
         quantise(GROUPS[0])
         linear_branch(PAIRS[2])
         turn(GROUPS[1], scalar)
-        first = second_product(PAIRS[0])
+        first_banks = second_product(PAIRS[0])
         gate(GROUPS[2])
         linear_branch(PAIRS[3])
         quantise(GROUPS[1])
-        store(PAIRS[0], first)
+        store(PAIRS[0], first_banks)
         turn(GROUPS[2], scalar)
-        second = second_product(PAIRS[1])
+        second_banks = second_product(PAIRS[1])
         gate(GROUPS[3])
         gate(GROUPS[4])
         quantise(GROUPS[2])
-        store(PAIRS[1], second)
+        store(PAIRS[1], second_banks)
         turn(GROUPS[3], scalar)
         turn(GROUPS[4], vector)
         quantise(GROUPS[3])
         quantise(GROUPS[4])
-        last_results()
+        last_results(PAIRS[2] + PAIRS[3])

@@ -28,8 +28,8 @@ X_LOADS = [(0, 256, 384), (384, 472, 512)]
 X_QUANTISED = [(0, 256), (256, 384), (384, 512)]
 PAIRS = [(0, 1), (2, 3), (4, 5), (6, 7)]
 GROUPS = [(0, 1), (2, 3), (4, 5), (6,), (7,)]
-GATHERS = PAIRS
-HELD = E
+GATHERS = [(0,), (1,), (2, 3), (4, 5), (6,), (7,)]
+HELD = E - 1
 
 
 def tile_moe_eps_glu_sigmoid_kernel(
@@ -77,16 +77,17 @@ def tile_moe_eps_glu_sigmoid_kernel(
                 nc.sync.dma_start(out=tile[:].bitcast(I32)[low:P:32], in_=rows[low])
 
         load_scales(w1_sc, w1_scales)
-        load_words(w1, "w1", w1_words, PAIRS[0] + PAIRS[1])
+        load_words(w1, "w1", w1_words, PAIRS[0])
+        load_words(w1, "w1", w1_words, PAIRS[1])
         load_scales(w3_sc, w3_scales)
-        load_scales(w2_sc[0], w2_scales[: E // 2])
         load_words(w3, "w3", w3_words, PAIRS[0])
         load_words(w1, "w1", w1_words, PAIRS[2])
         load_words(w3, "w3", w3_words, PAIRS[1])
         load_words(w1, "w1", w1_words, PAIRS[3])
         load_words(w3, "w3", w3_words, PAIRS[2])
-        load_words(w3, "w3", w3_words, PAIRS[3])
+        load_scales(w2_sc[0], w2_scales[: E // 2])
         load_words(w2, "w2", w2_words, PAIRS[0])
+        load_words(w3, "w3", w3_words, PAIRS[3])
         load_words(w2, "w2", w2_words, PAIRS[1])
         load_scales(w2_sc[1], w2_scales[E // 2 :])
         load_words(w2, "w2", w2_words, PAIRS[2] + PAIRS[3])
@@ -148,9 +149,9 @@ def tile_moe_eps_glu_sigmoid_kernel(
                     nc.vector.tensor_tensor(h[group][:, place, part], b[:, part], sig[e][:, part], MULT)
                 free_banks.append(b_bank[e])
 
-        def turn(group, copy):
+        def turn(group, copy, bank=None):
             size = len(group)
-            bank = free_banks.pop(0)
+            bank = free_banks.pop([bank is None or bank is free for free in free_banks].index(True))
             turned = bank[:, : size * 2 * P].rearrange("p (e u c) -> p e u c", e=size, u=2)
             pairs_of_i = h[group][:].rearrange("p e u q d -> p (e u q d)").bitcast(F32)
             for place in range(size):
@@ -235,32 +236,33 @@ def tile_moe_eps_glu_sigmoid_kernel(
 
         scalar, vector = nc.scalar.copy, nc.vector.tensor_copy
 
-        for experts in GATHERS:
+        for experts in GATHERS[:-1]:
             gather(experts)
         sigmoid_branch(PAIRS[0])
         sigmoid_branch(PAIRS[1])
         linear_branch(PAIRS[0])
         sigmoid_branch(PAIRS[2])
-        linear_branch(PAIRS[1])
         gate(GROUPS[0])
+        linear_branch(PAIRS[1])
+        gather(GATHERS[-1])
         turn(GROUPS[0], scalar)
         gate(GROUPS[1])
         sigmoid_branch(PAIRS[3])
-        quantise(GROUPS[0])
         linear_branch(PAIRS[2])
+        quantise(GROUPS[0])
         turn(GROUPS[1], scalar)
         first_banks = second_product(PAIRS[0])
         gate(GROUPS[2])
         linear_branch(PAIRS[3])
         quantise(GROUPS[1])
         store(PAIRS[0], first_banks)
-        turn(GROUPS[2], scalar)
+        turn(GROUPS[2], scalar, first_banks[0])
         second_banks = second_product(PAIRS[1])
         gate(GROUPS[3])
         gate(GROUPS[4])
+        turn(GROUPS[3], vector)
         quantise(GROUPS[2])
         store(PAIRS[1], second_banks)
-        turn(GROUPS[3], scalar)
         turn(GROUPS[4], vector)
         quantise(GROUPS[3])
         quantise(GROUPS[4])

@@ -184,26 +184,27 @@ def tile_moe_eps_glu_sigmoid_kernel(
             )
 
         def second_product(pair):
-            banks = [free_banks.pop(0) for e in pair]
-            for bank, e in zip(banks, pair):
-                for m in range(N_TILES):
-                    result_block(bank, m * C, e, m)
+            banks = [free_banks.pop(0), free_banks.pop(0)]
+            for m in range(N_TILES):
+                for place, e in enumerate(pair):
+                    result_block(banks[min(m, 1)], (max(m - 1, 0) * len(pair) + place) * C, e, m)
             return banks
 
         def store(pair, banks):
-            staged = keep.tile([P, N_TILES, R, len(pair), WIDTH], F32, name=f"staged{pair[0]}")
-            for place, bank in enumerate(banks):
+            size = len(pair)
+            for bank, blocks in zip(banks, (range(0, 1), range(1, N_TILES))):
+                staged = keep.tile([P, len(blocks), R, size, WIDTH], F32, name=f"staged{pair[0]}_{blocks[0]}")
                 nc.scalar.copy(
-                    out=staged[:, :, :, place, :],
-                    in_=bank[:, : N_TILES * C].rearrange("p (m r c) -> p m r c", r=R, c=WIDTH),
+                    out=staged[:],
+                    in_=bank[:, : len(blocks) * size * C].rearrange("p (m e r c) -> p m r e c", e=size, r=R, c=WIDTH),
                 )
                 free_banks.append(bank)
-            for r in range(R):
-                column = r * (SLOTS // R) + pair[0] * WIDTH
-                nc.sync.dma_start(
-                    out=out[:, column : column + len(pair) * WIDTH].rearrange("(m p) w -> p m w", p=P),
-                    in_=staged[:, :, r, :, :].rearrange("p m e c -> p m (e c)"),
-                )
+                for place, m in enumerate(blocks):
+                    rows = out[m * P : (m + 1) * P, :].rearrange("p (r w) -> p r w", r=R)
+                    nc.sync.dma_start(
+                        out=rows[:, :, pair[0] * WIDTH : (pair[-1] + 1) * WIDTH],
+                        in_=staged[:, place].rearrange("p r e c -> p r (e c)"),
+                    )
 
         def last_results(experts):
             size = len(experts)
@@ -260,8 +261,8 @@ def tile_moe_eps_glu_sigmoid_kernel(
         second_banks = second_product(PAIRS[1])
         gate(GROUPS[3])
         gate(GROUPS[4])
-        turn(GROUPS[3], vector)
         quantise(GROUPS[2])
+        turn(GROUPS[3], vector)
         store(PAIRS[1], second_banks)
         turn(GROUPS[4], vector)
         quantise(GROUPS[3])

@@ -231,7 +231,8 @@ def tile_moe_eps_glu_sigmoid_kernel(
             stage(vector, banks[2], 2, 0, size)
             for m in range(N_TILES):
                 rows = out[m * P : (m + 1) * P, :].rearrange("p (r w) -> p r w", r=R)
-                nc.sync.dma_start(
+                queue = nc.scalar if m == 1 else nc.sync
+                queue.dma_start(
                     out=rows[:, :, experts[0] * WIDTH :], in_=staged[m][:].rearrange("p r e c -> p r (e c)")
                 )
 

from contextlib import ExitStack

import concourse.mybir as mybir
from concourse.masks import make_identity

P = 128
PACK = 4
K, T, E, C, H, N = 512, 512, 8, 128, 512, 384
R = 2
SLOTS = E * C
N_TILES = N // P
WIDTH = C // R
BANKS = 8
FLOPS = 2 * SLOTS * (2 * K * H + H * N)

F32 = mybir.dt.float32
BF16 = mybir.dt.bfloat16
I32 = mybir.dt.int32
U32 = mybir.dt.uint32
U16 = mybir.dt.uint16
U8 = mybir.dt.uint8
FP8X4 = mybir.dt.float8_e4m3fn_x4
FP4X4 = mybir.dt.float4_e2m1fn_x4
MULT = mybir.AluOpType.mult
SIGMOID = mybir.ActivationFunctionType.Sigmoid

X_LOADS = [(0, 256, 384), (384, 472, 512)]
X_QUANTISED = [(0, 256), (256, 384), (384, 512)]
PAIRS = [(0, 1), (2, 3), (4, 5), (6, 7)]
GROUPS = [(0, 1), (2, 3), (4, 5), (6,), (7,)]
GATHERS = [(0,), (1,), (2, 3), (4, 5), (6,), (7,)]
HELD = E - 1


def tile_moe_eps_glu_sigmoid_kernel(
    tc, xT, w1_words, w1_scales, w3_words, w3_scales, w2_words, w2_scales, offs, out
):
    nc = tc.nc
    with ExitStack() as ctx:
        keep = ctx.enter_context(tc.tile_pool(name="keep", bufs=1))
        psum = ctx.enter_context(tc.psum_pool(name="psum", bufs=1))

        offsets = keep.tile([P, SLOTS // 16], U16, name="offsets")
        x_raw = [keep.tile([P, PACK, end - start], F32, name=f"x_raw{start}") for start, split, end in X_LOADS]
        x_grouped = keep.tile([P, T, PACK], BF16, name="x_grouped", align_bytes=64)
        x_codes = keep.tile([P, T], U32, name="x_codes", align_bytes=64)
        x_scales = keep.tile([P, T], U8, name="x_scales", align_bytes=64)
        slot_codes = keep.tile([P, HELD * C], U32, name="slot_codes", align_bytes=64)
        slot_scales = keep.tile([P, HELD * C], U8, name="slot_scales", align_bytes=64)
        w1_sc = keep.tile([P, E, H], U8, name="w1_sc", align_bytes=64)
        w3_sc = keep.tile([P, E, H], U8, name="w3_sc", align_bytes=64)
        w2_sc = [keep.tile([P, E // 2, N], U8, name=f"w2_sc{half}", align_bytes=64) for half in range(2)]
        ident = keep.tile([P, P], F32, name="ident")
        free_banks = [psum.tile([P, H], F32, name=f"bank{number}") for number in range(BANKS)]

        for raw, (start, split, end) in zip(x_raw, X_LOADS):
            nc.sync.dma_start(out=raw[:], in_=xT[:, start:end].rearrange("(p t) w -> p t w", t=PACK))
        nc.sync.dma_start(offsets[:], offs)

        for scale_tile in (w1_sc, x_scales, w3_sc, *w2_sc):
            nc.vector.memset(scale_tile[:].bitcast(I32), 0)
        make_identity(nc, ident[:])

        w1, w3, w2 = {}, {}, {}

        def load_words(table, name, words, experts):
            tile = keep.tile([P, len(experts), words.shape[3]], U8, name=f"{name}_{experts[0]}", align_bytes=64)
            nc.sync.dma_start(
                out=tile[:].bitcast(I32),
                in_=words[experts[0] : experts[-1] + 1].bitcast(I32).rearrange("e s p w -> p (e s) w"),
            )
            table.update({e: tile[:, place, :] for place, e in enumerate(experts)})

        def load_scales(tile, scales):
            rows = scales.bitcast(I32).rearrange("e s (high low) w -> low high (e s) w", low=4)
            for low in range(4):
                nc.sync.dma_start(out=tile[:].bitcast(I32)[low:P:32], in_=rows[low])

        load_scales(w1_sc, w1_scales)
        load_words(w1, "w1", w1_words, PAIRS[0])
        load_words(w1, "w1", w1_words, PAIRS[1])
        load_scales(w3_sc, w3_scales)
        load_words(w3, "w3", w3_words, PAIRS[0])
        load_words(w1, "w1", w1_words, PAIRS[2])
        load_words(w3, "w3", w3_words, PAIRS[1])
        load_words(w1, "w1", w1_words, PAIRS[3])
        load_words(w3, "w3", w3_words, PAIRS[2])
        load_scales(w2_sc[0], w2_scales[: E // 2])
        load_words(w2, "w2", w2_words, PAIRS[0])
        load_words(w3, "w3", w3_words, PAIRS[3])
        load_words(w2, "w2", w2_words, PAIRS[1])
        load_scales(w2_sc[1], w2_scales[E // 2 :])
        load_words(w2, "w2", w2_words, PAIRS[2] + PAIRS[3])

        for raw, (start, split, end) in zip(x_raw, X_LOADS):
            nc.scalar.copy(out=x_grouped[:, split:end, :], in_=raw[:, :, split - start :].rearrange("p t w -> p w t"))
            nc.vector.tensor_copy(
                out=x_grouped[:, start:split, :], in_=raw[:, :, : split - start].rearrange("p t w -> p w t")
            )
        for start, end in X_QUANTISED:
            nc.vector.quantize_mx(
                out=x_codes[:, start:end].bitcast(FP8X4),
                scales=x_scales[:, start:end],
                in_=x_grouped[:, start:end, :].rearrange("p w t -> p (w t)"),
            )

        sig, b_bank, h, hT, h_codes, h_scales = {}, {}, {}, {}, {}, {}

        def held_columns(experts):
            return slice(experts[0] % HELD * C, (experts[-1] % HELD + 1) * C)

        def place_in_group(e):
            return [(group, group.index(e)) for group in GROUPS if e in group][0]

        def gather(experts):
            entries = offsets[:, experts[0] * C // 16 : (experts[-1] + 1) * C // 16]
            nc.vector.tensor_copy(out=slot_codes[:, held_columns(experts)], in_=x_codes[:].indirect(entries))
            nc.vector.tensor_copy(out=slot_scales[:, held_columns(experts)], in_=x_scales[:].indirect(entries))

        def first_product(e, words, scale_tile):
            bank = free_banks.pop(0)
            nc.tensor.matmul_mx(
                out=bank[:],
                lhsT=slot_codes[:, held_columns([e])].bitcast(FP8X4),
                lhsT_scale=slot_scales[:, held_columns([e])],
                rhs=words[e].bitcast(FP4X4),
                rhs_scale=scale_tile[:, e, :],
                start=True,
                stop=True,
            )
            return bank

        def sigmoid_branch(experts):
            for e in experts:
                bank = first_product(e, w1, w1_sc)
                sig[e] = keep.tile([P, 2, P, 2], F32, name=f"sig{e}")
                nc.scalar.activation(sig[e][:], bank[:].rearrange("p (q u d) -> p u q d", u=2, d=2), SIGMOID)
                free_banks.append(bank)

        def linear_branch(experts):
            for e in experts:
                b_bank[e] = first_product(e, w3, w3_sc)

        def gate(group):
            h[group] = keep.tile([P, len(group), 2, P, 2], BF16, name=f"h{group[0]}")
            for place, e in enumerate(group):
                b = b_bank[e][:].rearrange("p (q u d) -> p u q d", u=2, d=2)
                for part in (slice(0, 1), slice(1, 2)) if e == E - 1 else (slice(0, 2),):
                    nc.vector.tensor_tensor(h[group][:, place, part], b[:, part], sig[e][:, part], MULT)
                free_banks.append(b_bank[e])

        def turn(group, copy, bank=None):
            size = len(group)
            bank = free_banks.pop([bank is None or bank is free for free in free_banks].index(True))
            turned = bank[:, : size * 2 * P].rearrange("p (e u c) -> p e u c", e=size, u=2)
            pairs_of_i = h[group][:].rearrange("p e u q d -> p (e u q d)").bitcast(F32)
            for place in range(size):
                for u in range(2):
                    column = (2 * place + u) * P
                    nc.tensor.transpose(turned[:, place, u, :], pairs_of_i[:, column : column + P], ident[:])
            hT[group] = keep.tile([P, size * C * PACK], BF16, name=f"hT{group[0]}", align_bytes=64)
            copy(
                out=hT[group][:].bitcast(F32).rearrange("p (e c u) -> p e c u", e=size, u=2),
                in_=turned.rearrange("p e u c -> p e c u"),
            )
            free_banks.append(bank)

        def quantise(group):
            size = len(group)
            h_codes[group] = keep.tile([P, size * C], U32, name=f"h_codes{group[0]}", align_bytes=64)
            h_scales[group] = keep.tile([P, size * C], U8, name=f"h_scales{group[0]}", align_bytes=64)
            nc.vector.quantize_mx(out=h_codes[group][:].bitcast(FP8X4), scales=h_scales[group][:], in_=hT[group][:])

        def result_block(bank, column, e, m):
            group, place = place_in_group(e)
            nc.tensor.matmul_mx(
                out=bank[:, column : column + C],
                lhsT=w2[e][:, 2 * P * m : 2 * P * (m + 1)].bitcast(FP4X4),
                lhsT_scale=w2_sc[e // (E // 2)][:, e % (E // 2), P * m : P * (m + 1)],
                rhs=h_codes[group][:, place * C : (place + 1) * C].bitcast(FP8X4),
                rhs_scale=h_scales[group][:, place * C : (place + 1) * C],
                start=True,
                stop=True,
            )

        def second_product(pair):
            banks = [free_banks.pop(0), free_banks.pop(0)]
            for m in range(N_TILES):
                for place, e in enumerate(pair):
                    result_block(banks[min(m, 1)], (max(m - 1, 0) * len(pair) + place) * C, e, m)
            return banks

        def store(pair, banks):
            size = len(pair)
            for bank, blocks in zip(banks, (range(0, 1), range(1, N_TILES))):
                staged = keep.tile([P, len(blocks), R, size, WIDTH], F32, name=f"staged{pair[0]}_{blocks[0]}")
                nc.scalar.copy(
                    out=staged[:],
                    in_=bank[:, : len(blocks) * size * C].rearrange("p (m e r c) -> p m r e c", e=size, r=R, c=WIDTH),
                )
                free_banks.append(bank)
                for place, m in enumerate(blocks):
                    rows = out[m * P : (m + 1) * P, :].rearrange("p (r w) -> p r w", r=R)
                    nc.sync.dma_start(
                        out=rows[:, :, pair[0] * WIDTH : (pair[-1] + 1) * WIDTH],
                        in_=staged[:, place].rearrange("p r e c -> p r (e c)"),
                    )

        def last_results(experts):
            size = len(experts)
            banks = [free_banks.pop(0) for m in range(N_TILES)]
            apart = free_banks.pop(0)
            early = [(place, m) for m in range(N_TILES - 1) for place in range(size // 2)]
            rest = [(place, m) for m in range(N_TILES) for place in range(size) if (place, m) not in early]
            for place, m in early + rest:
                if (place, m) == (size - 1, 0):
                    result_block(apart, 0, experts[place], m)
                else:
                    result_block(banks[m], place * C, experts[place], m)
            staged = [keep.tile([P, R, size, WIDTH], F32, name=f"last{m}") for m in range(N_TILES)]

            def stage(copy, bank, m, start, end):
                copy(
                    out=staged[m][:, :, start:end, :],
                    in_=bank[:, : (end - start) * C].rearrange("p (e r c) -> p r e c", r=R, c=WIDTH),
                )

            stage(scalar, banks[0], 0, 0, size - 1)
            stage(vector, apart, 0, size - 1, size)
            stage(scalar, banks[1], 1, 0, size)
            stage(vector, banks[2], 2, 0, size)
            for m in range(N_TILES):
                rows = out[m * P : (m + 1) * P, :].rearrange("p (r w) -> p r w", r=R)
                queue = nc.scalar if m == 1 else nc.sync
                queue.dma_start(
                    out=rows[:, :, experts[0] * WIDTH :], in_=staged[m][:].rearrange("p r e c -> p r (e c)")
                )

        scalar, vector = nc.scalar.copy, nc.vector.tensor_copy

        for experts in GATHERS[:-1]:
            gather(experts)
        sigmoid_branch(PAIRS[0])
        sigmoid_branch(PAIRS[1])
        linear_branch(PAIRS[0])
        sigmoid_branch(PAIRS[2])
        gate(GROUPS[0])
        linear_branch(PAIRS[1])
        gather(GATHERS[-1])
        turn(GROUPS[0], scalar)
        gate(GROUPS[1])
        sigmoid_branch(PAIRS[3])
        linear_branch(PAIRS[2])
        quantise(GROUPS[0])
        turn(GROUPS[1], scalar)
        first_banks = second_product(PAIRS[0])
        gate(GROUPS[2])
        linear_branch(PAIRS[3])
        quantise(GROUPS[1])
        store(PAIRS[0], first_banks)
        turn(GROUPS[2], scalar, first_banks[0])
        second_banks = second_product(PAIRS[1])
        gate(GROUPS[3])
        gate(GROUPS[4])
        quantise(GROUPS[2])
        turn(GROUPS[3], vector)
        store(PAIRS[1], second_banks)
        turn(GROUPS[4], vector)
        quantise(GROUPS[3])
        quantise(GROUPS[4])
        last_results(PAIRS[2] + PAIRS[3])
